import numpy as np
import ml_dtypes


def mxq(x, axis, fmt="e4m3"):
    dtype, down = {"e4m3": (ml_dtypes.float8_e4m3fn, 7), "e5m2": (ml_dtypes.float8_e5m2, 14)}[fmt]
    v = np.moveaxis(np.asarray(x, np.float32).astype(ml_dtypes.bfloat16).astype(np.float64), axis, -1)
    blocks = v.reshape(v.shape[:-1] + (-1, 32))
    amax = np.abs(blocks).max(-1, keepdims=True)
    byte = np.maximum(np.where(amax > 0, np.frexp(amax)[1] - 1 + 127, 0) - down, 1)
    scale = np.exp2(byte - 127.0)
    codes = (blocks / scale).astype(np.float32).astype(dtype).astype(np.float64)
    return np.moveaxis((codes * scale).reshape(v.shape), -1, axis)


WIDE = False


def mx_kscale(k):
    if not WIDE:
        return np.ones(k)
    levels = np.array([10, -10, 5, -5, 0])
    if k % 512:
        return np.exp2(np.random.permutation(np.resize(levels, k // 32))).repeat(32)
    a = np.empty((k // 512, 16))
    for p in range(k // 512):
        a[p, :8] = np.random.permutation(np.resize(levels, 8))
        for g in range(8):
            far = levels[np.abs(levels - a[p, g]) >= 10]
            a[p, g + 8] = far[np.random.randint(len(far))]
    return np.exp2(a.ravel()).repeat(32)


def f64(x):
    return np.asarray(x).astype(np.float64)


def striped(idx):
    return np.tile(idx.reshape(-1, 16).T, (8, 1)).astype(np.uint16)


def unstriped(offs):
    return offs[:16].T.reshape(-1).astype(np.int64)


E2M1 = np.array([0.0, 0.5, 1.0, 1.5, 2.0, 3.0, 4.0, 6.0, -0.0, -0.5, -1.0, -1.5, -2.0, -3.0, -4.0, -6.0])


def pack_weight(w, fmt):
    k, n = w.shape
    w = f64(np.asarray(w, np.float32).astype(ml_dtypes.bfloat16)).reshape(k // 32, 32, n)
    amax = np.abs(w).max(1)
    if fmt == "e4m3":
        byte = np.frexp(amax)[1] - 1 + 127 - 7
    else:
        mant, ex = np.frexp(amax / 6.0)
        byte = np.where(mant > 0.5, ex, ex - 1) + 127
    byte = np.clip(np.where(amax > 0, byte, 1), 1, 254)
    scaled = (w * np.exp2(127.0 - byte)[:, None, :]).reshape(k, n).astype(np.float32)
    by_word = np.ascontiguousarray(scaled.reshape(k // 512, 128, 4, n).transpose(0, 1, 3, 2))
    if fmt == "e4m3":
        words = by_word.astype(ml_dtypes.float8_e4m3fn).view(np.uint8)
    else:
        c = by_word.astype(ml_dtypes.float4_e2m1fn).view(np.uint8) & 0xF
        words = (c[..., 0::2] | (c[..., 1::2] << 4)).reshape(k // 512, 128, 2 * n)
    return np.ascontiguousarray(words), np.ascontiguousarray(byte.astype(np.uint8).reshape(k // 512, 16, n))


def unpack_weight(words, scales, fmt):
    g, _, n = scales.shape
    words = np.ascontiguousarray(words).reshape(g, 128, n, -1)
    if fmt == "e4m3":
        vals = words.view(ml_dtypes.float8_e4m3fn).astype(np.float64)
    else:
        nib = np.empty((g, 128, n, 4), np.uint8)
        nib[..., 0::2] = words & 0xF
        nib[..., 1::2] = words >> 4
        vals = E2M1[nib]
    vals = vals * np.repeat(np.exp2(scales.astype(np.float64) - 127.0), 8, axis=1)[..., None]
    return vals.transpose(0, 1, 3, 2).reshape(g * 512, n)


K, M, T, S = 512, 256, 4096, 1536


def setup_inputs():
    n = np.random.standard_normal
    s = mx_kscale(K)[:, None]
    u = mx_kscale(512)[:, None]
    v = pack_weight(n((K, T)) * s, "e4m3")
    p_w2 = pack_weight(1.4 * n((512, M)) / np.sqrt(512) / u, "e2m1")
    return {
        "tab_words": v[0],
        "tab_scales": v[1],
        "w1": (n((K, 512)) / np.sqrt(K) / s * u.T).astype(np.float32),
        "w2_words": p_w2[0],
        "w2_scales": p_w2[1],
        "gT": n((M, T)).astype(np.float32),
        "b": (0.3 * n(256)).astype(np.float32),
        "offs": striped(np.random.permutation(T)[:S]),
    }


def reference(tab_words, tab_scales, w1, w2_words, w2_scales, gT, b, offs):
    tab_ = unpack_weight(tab_words, tab_scales, "e4m3")[:, unstriped(offs)]
    w1_ = mxq(f64(w1), 0, "e4m3")
    w2_ = unpack_weight(w2_words, w2_scales, "e2m1")
    h_ = mxq(np.maximum(w1_.T @ tab_, 0.0), 0, "e4m3")
    y = w2_.T @ h_
    return (y + f64(b)[:, None]) * f64(gT)[:, unstriped(offs)]

@@ -1,0 +1,168 @@
+from contextlib import ExitStack
+
+import concourse.mybir as mybir
+
+K, R, M, T, S = 512, 512, 256, 4096, 1536
+FLOPS = 2 * K * R * S + 2 * R * M * S
+
+F32 = mybir.dt.float32
+BF16 = mybir.dt.bfloat16
+I32 = mybir.dt.int32
+U32 = mybir.dt.uint32
+U16 = mybir.dt.uint16
+U8 = mybir.dt.uint8
+FP8X4 = mybir.dt.float8_e4m3fn_x4
+FP4X4 = mybir.dt.float4_e2m1fn_x4
+ACT = mybir.ActivationFunctionType
+ALU = mybir.AluOpType
+
+P = 128
+PACK = 4
+CHUNK = 512
+GROUP = 128
+LANES = 16
+
+
+def tile_list_tabgate_bias_kernel(tc, tab_words, tab_scales, w1, w2_words, w2_scales, gT, b, offs, out):
+    nc = tc.nc
+    with ExitStack() as ctx:
+        keep = ctx.enter_context(tc.tile_pool(name="keep", bufs=1))
+        psum_h = ctx.enter_context(tc.psum_pool(name="psum_h", bufs=4))
+        psum_y = ctx.enter_context(tc.psum_pool(name="psum_y", bufs=4))
+
+        offsets = keep.tile([P, S // LANES], U16, name="offsets")
+        nc.sync.dma_start(offsets[:], offs)
+
+        w1_raw = keep.tile([P, PACK, R], F32, name="w1_raw")
+        nc.sync.dma_start(w1_raw[:], w1.rearrange("(p j) c -> p j c", j=PACK))
+
+        tab_sc = keep.tile([P, T], U8, name="tab_sc", align_bytes=64)
+        nc.vector.memset(tab_sc[:].bitcast(I32), 0)
+        for q in range(4):
+            nc.scalar.dma_start(tab_sc[32 * q : 32 * q + 4, :].bitcast(I32), tab_scales[0, 4 * q : 4 * q + 4, :].bitcast(I32))
+
+        tab_w = keep.tile([P, T], U32, name="tab_w", align_bytes=64)
+        nc.sync.dma_start(tab_w[:].bitcast(I32), tab_words[0].rearrange("p t i -> p (t i)").bitcast(I32))
+
+        gates = []
+        for half in range(2):
+            g = keep.tile([P, T], F32, name="gate%d" % half, align_bytes=64)
+            nc.sync.dma_start(g[:], gT[half * P : (half + 1) * P, :])
+            gates.append(g)
+
+        w2_w = keep.tile([P, 2 * M], U8, name="w2_w", align_bytes=64)
+        w2_sc = keep.tile([P, M], U8, name="w2_sc", align_bytes=64)
+        bias = keep.tile([P, 2], F32, name="bias")
+        nc.gpsimd.memset(w2_sc[:], 0)
+        nc.gpsimd.dma_start(w2_w[:].bitcast(I32), w2_words[0].bitcast(I32))
+        for q in range(4):
+            nc.gpsimd.dma_start(w2_sc[32 * q : 32 * q + 4, :].bitcast(I32), w2_scales[0, 4 * q : 4 * q + 4, :].bitcast(I32))
+        with nc.allow_non_contiguous_dma(reason="one bias value for each partition"):
+            nc.gpsimd.dma_start(bias[:], b.rearrange("(h p) -> p h", p=P))
+
+        v_sc = keep.tile([P, S], U8, name="v_sc", align_bytes=64)
+        nc.vector.tensor_copy(v_sc[:], tab_sc[:].indirect(offsets[:]))
+
+        w1_bf = keep.tile([P, PACK * R], BF16, name="w1_bf", align_bytes=64)
+        nc.scalar.copy(
+            w1_bf[:].rearrange("p (t m j) -> p m t j", t=PACK, j=PACK),
+            w1_raw[:].rearrange("p j (m t) -> p m t j", t=PACK),
+        )
+        w1_q = keep.tile([P, R], U32, name="w1_q", align_bytes=64)
+        w1_sc = keep.tile([P, R], U8, name="w1_sc", align_bytes=64)
+        nc.vector.quantize_mx(out=w1_q[:].bitcast(FP8X4), scales=w1_sc[:], in_=w1_bf[:])
+
+        def listed(first, count):
+            return offsets[:, first // LANES : (first + count) // LANES]
+
+        v_w = []
+        for c in range(S // CHUNK):
+            vw = keep.tile([P, CHUNK], U32, name="v_w%d" % c, align_bytes=64)
+            nc.vector.tensor_copy(vw[:], tab_w[:].indirect(listed(c * CHUNK, CHUNK)))
+            v_w.append(vw)
+
+        h_bf = [keep.tile([P, PACK * CHUNK], BF16, name="h_bf%d" % c, align_bytes=64) for c in range(S // CHUNK)]
+        h_q = [keep.tile([P, CHUNK], U32, name="h_q%d" % c, align_bytes=64) for c in range(S // CHUNK)]
+        h_sc = [keep.tile([P, CHUNK], U8, name="h_sc%d" % c, align_bytes=64) for c in range(S // CHUNK)]
+        y_ps = {}
+        y_sb = {}
+
+        def hidden(group, on_vector=False):
+            c, i = divmod(group, CHUNK // GROUP)
+            bank = psum_h.tile([P, PACK, GROUP], F32, name="h_bank")
+            for t in range(PACK):
+                nc.tensor.matmul_mx(
+                    out=bank[:, t, :],
+                    lhsT=w1_q[:, t * P : (t + 1) * P].bitcast(FP8X4),
+                    lhsT_scale=w1_sc[:, t * P : (t + 1) * P],
+                    rhs=v_w[c][:, i * GROUP : (i + 1) * GROUP].bitcast(FP8X4),
+                    rhs_scale=v_sc[:, group * GROUP : (group + 1) * GROUP],
+                    start=True,
+                    stop=True,
+                )
+            dst = h_bf[c][:, i * GROUP * PACK : (i + 1) * GROUP * PACK].rearrange("p (n t) -> p n t", t=PACK)
+            src = bank[:].rearrange("p t n -> p n t")
+            if on_vector:
+                nc.vector.tensor_scalar_max(dst, src, 0.0)
+            else:
+                nc.scalar.activation(dst, src, ACT.Relu)
+
+        def quantize_hidden(c):
+            nc.vector.quantize_mx(out=h_q[c][:].bitcast(FP8X4), scales=h_sc[c][:], in_=h_bf[c][:])
+
+        def project(c):
+            for half in range(2):
+                bank = psum_y.tile([P, CHUNK], F32, name="y_bank")
+                nc.tensor.matmul_mx(
+                    out=bank[:],
+                    lhsT=w2_w[:, 2 * half * P : 2 * (half + 1) * P].bitcast(FP4X4),
+                    lhsT_scale=w2_sc[:, half * P : (half + 1) * P],
+                    rhs=h_q[c][:].bitcast(FP8X4),
+                    rhs_scale=h_sc[c][:],
+                    start=True,
+                    stop=True,
+                )
+                y_ps[c, half] = bank
+
+        def add_bias(c, half):
+            y = keep.tile([P, CHUNK], F32, name="y%d_%d" % (c, half))
+            nc.scalar.activation(y[:], y_ps[c, half][:], ACT.Identity, bias=bias[:, half : half + 1])
+            y_sb[c, half] = y
+
+        def gate(c, half, widths=(CHUNK,)):
+            first = 0
+            for width in widths:
+                res = keep.tile([P, width], F32, name="res%d_%d_%d" % (c, half, first))
+                token = c * CHUNK + first
+                nc.vector.tensor_tensor(res[:], gates[half][:].indirect(listed(token, width)), y_sb[c, half][:, first : first + width], ALU.mult)
+                nc.sync.dma_start(out[half * P : (half + 1) * P, token : token + width], res[:])
+                first += width
+
+        for group in range(4):
+            hidden(group)
+        quantize_hidden(0)
+        hidden(4)
+        hidden(5)
+        hidden(6, on_vector=True)
+        hidden(7, on_vector=True)
+        project(0)
+        add_bias(0, 0)
+        quantize_hidden(1)
+        hidden(8)
+        hidden(9)
+        gate(0, 0)
+        project(1)
+        add_bias(1, 0)
+        hidden(10)
+        hidden(11)
+        gate(1, 0)
+        quantize_hidden(2)
+        add_bias(0, 1)
+        project(2)
+        add_bias(2, 0)
+        gate(0, 1)
+        add_bias(1, 1)
+        gate(2, 0)
+        add_bias(2, 1)
+        gate(1, 1)
+        gate(2, 1, widths=(256, 256))

@@ -34,31 +34,38 @@ def tile_list_tabgate_bias_kernel(tc, tab_words, tab_scales, w1, w2_words, w2_sc
         nc.sync.dma_start(offsets[:], offs)
 
         w1_raw = keep.tile([P, PACK, R], F32, name="w1_raw")
-        nc.sync.dma_start(w1_raw[:], w1.rearrange("(p j) c -> p j c", j=PACK))
+        w1_rows = w1.rearrange("(p j) c -> p j c", j=PACK)
+        nc.sync.dma_start(w1_raw[:, 0:2, :], w1_rows[:, 0:2, :])
 
         tab_sc = keep.tile([P, T], U8, name="tab_sc", align_bytes=64)
         nc.vector.memset(tab_sc[:].bitcast(I32), 0)
         for q in range(4):
-            nc.scalar.dma_start(tab_sc[32 * q : 32 * q + 4, :].bitcast(I32), tab_scales[0, 4 * q : 4 * q + 4, :].bitcast(I32))
+            nc.sync.dma_start(tab_sc[32 * q : 32 * q + 4, :].bitcast(I32), tab_scales[0, 4 * q : 4 * q + 4, :].bitcast(I32))
+
+        nc.sync.dma_start(w1_raw[:, 2:4, :], w1_rows[:, 2:4, :])
 
         tab_w = keep.tile([P, T], U32, name="tab_w", align_bytes=64)
         nc.sync.dma_start(tab_w[:].bitcast(I32), tab_words[0].rearrange("p t i -> p (t i)").bitcast(I32))
 
-        gates = []
-        for half in range(2):
-            g = keep.tile([P, T], F32, name="gate%d" % half, align_bytes=64)
-            nc.sync.dma_start(g[:], gT[half * P : (half + 1) * P, :])
-            gates.append(g)
+        gates = [keep.tile([P, T], F32, name="gate%d" % half, align_bytes=64) for half in range(2)]
+        nc.sync.dma_start(gates[0][:], gT[0:P, :])
 
         w2_w = keep.tile([P, 2 * M], U8, name="w2_w", align_bytes=64)
         w2_sc = keep.tile([P, M], U8, name="w2_sc", align_bytes=64)
         bias = keep.tile([P, 2], F32, name="bias")
         nc.gpsimd.memset(w2_sc[:], 0)
-        nc.gpsimd.dma_start(w2_w[:].bitcast(I32), w2_words[0].bitcast(I32))
+        nc.sync.dma_start(w2_w[:].bitcast(I32), w2_words[0].bitcast(I32))
         for q in range(4):
-            nc.gpsimd.dma_start(w2_sc[32 * q : 32 * q + 4, :].bitcast(I32), w2_scales[0, 4 * q : 4 * q + 4, :].bitcast(I32))
+            nc.sync.dma_start(w2_sc[32 * q : 32 * q + 4, :].bitcast(I32), w2_scales[0, 4 * q : 4 * q + 4, :].bitcast(I32))
         with nc.allow_non_contiguous_dma(reason="one bias value for each partition"):
-            nc.gpsimd.dma_start(bias[:], b.rearrange("(h p) -> p h", p=P))
+            nc.sync.dma_start(bias[:], b.rearrange("(h p) -> p h", p=P))
+
+        nc.sync.dma_start(gates[1][:], gT[P : 2 * P, :])
+
+        warm_in = keep.tile([P, 1], F32, name="warm_in")
+        warm_out = keep.tile([P, 1], F32, name="warm_out")
+        nc.gpsimd.memset(warm_in[:], 0.0)
+        nc.scalar.activation(warm_out[:], warm_in[:], ACT.Relu)
 
         v_sc = keep.tile([P, S], U8, name="v_sc", align_bytes=64)
         nc.vector.tensor_copy(v_sc[:], tab_sc[:].indirect(offsets[:]))
@@ -110,19 +117,18 @@ def tile_list_tabgate_bias_kernel(tc, tab_words, tab_scales, w1, w2_words, w2_sc
         def quantize_hidden(c):
             nc.vector.quantize_mx(out=h_q[c][:].bitcast(FP8X4), scales=h_sc[c][:], in_=h_bf[c][:])
 
-        def project(c):
-            for half in range(2):
-                bank = psum_y.tile([P, CHUNK], F32, name="y_bank")
-                nc.tensor.matmul_mx(
-                    out=bank[:],
-                    lhsT=w2_w[:, 2 * half * P : 2 * (half + 1) * P].bitcast(FP4X4),
-                    lhsT_scale=w2_sc[:, half * P : (half + 1) * P],
-                    rhs=h_q[c][:].bitcast(FP8X4),
-                    rhs_scale=h_sc[c][:],
-                    start=True,
-                    stop=True,
-                )
-                y_ps[c, half] = bank
+        def project(c, half):
+            bank = psum_y.tile([P, CHUNK], F32, name="y_bank")
+            nc.tensor.matmul_mx(
+                out=bank[:],
+                lhsT=w2_w[:, 2 * half * P : 2 * (half + 1) * P].bitcast(FP4X4),
+                lhsT_scale=w2_sc[:, half * P : (half + 1) * P],
+                rhs=h_q[c][:].bitcast(FP8X4),
+                rhs_scale=h_sc[c][:],
+                start=True,
+                stop=True,
+            )
+            y_ps[c, half] = bank
 
         def add_bias(c, half):
             y = keep.tile([P, CHUNK], F32, name="y%d_%d" % (c, half))
@@ -138,31 +144,36 @@ def tile_list_tabgate_bias_kernel(tc, tab_words, tab_scales, w1, w2_words, w2_sc
                 nc.sync.dma_start(out[half * P : (half + 1) * P, token : token + width], res[:])
                 first += width
 
-        for group in range(4):
-            hidden(group)
+        hidden(0)
+        hidden(1)
+        hidden(2)
+        hidden(3, on_vector=True)
         quantize_hidden(0)
         hidden(4)
         hidden(5)
-        hidden(6, on_vector=True)
+        hidden(6)
         hidden(7, on_vector=True)
-        project(0)
-        add_bias(0, 0)
+        project(0, 0)
         quantize_hidden(1)
         hidden(8)
-        hidden(9)
-        gate(0, 0)
-        project(1)
-        add_bias(1, 0)
+        hidden(9, on_vector=True)
+        add_bias(0, 0)
         hidden(10)
         hidden(11)
-        gate(1, 0)
+        gate(0, 0)
+        project(1, 0)
         quantize_hidden(2)
+        add_bias(1, 0)
+        project(0, 1)
+        project(1, 1)
+        gate(1, 0)
         add_bias(0, 1)
-        project(2)
-        add_bias(2, 0)
-        gate(0, 1)
         add_bias(1, 1)
-        gate(2, 0)
-        add_bias(2, 1)
+        project(2, 0)
+        project(2, 1)
+        gate(0, 1)
+        add_bias(2, 0)
         gate(1, 1)
-        gate(2, 1, widths=(256, 256))
+        add_bias(2, 1)
+        gate(2, 0)
+        gate(2, 1, widths=(384, 128))

@@ -27,20 +27,21 @@ def tile_list_tabgate_bias_kernel(tc, tab_words, tab_scales, w1, w2_words, w2_sc
     nc = tc.nc
     with ExitStack() as ctx:
         keep = ctx.enter_context(tc.tile_pool(name="keep", bufs=1))
+        reuse = ctx.enter_context(tc.tile_pool(name="reuse", bufs=1))
         psum_h = ctx.enter_context(tc.psum_pool(name="psum_h", bufs=4))
         psum_y = ctx.enter_context(tc.psum_pool(name="psum_y", bufs=4))
 
         offsets = keep.tile([P, S // LANES], U16, name="offsets")
         nc.sync.dma_start(offsets[:], offs)
 
-        w1_raw = keep.tile([P, PACK, R], F32, name="w1_raw")
+        w1_raw = reuse.tile([P, PACK, R], F32, name="w1_raw", offset=0)
         w1_rows = w1.rearrange("(p j) c -> p j c", j=PACK)
         nc.sync.dma_start(w1_raw[:, 0:2, :], w1_rows[:, 0:2, :])
 
         tab_sc = keep.tile([P, T], U8, name="tab_sc", align_bytes=64)
         nc.vector.memset(tab_sc[:].bitcast(I32), 0)
         for q in range(4):
-            nc.sync.dma_start(tab_sc[32 * q : 32 * q + 4, :].bitcast(I32), tab_scales[0, 4 * q : 4 * q + 4, :].bitcast(I32))
+            nc.sync.dma_start(tab_sc[q:P:32, :].bitcast(I32), tab_scales[0, q:16:4, :].bitcast(I32))
 
         nc.sync.dma_start(w1_raw[:, 2:4, :], w1_rows[:, 2:4, :])
 
@@ -49,16 +50,6 @@ def tile_list_tabgate_bias_kernel(tc, tab_words, tab_scales, w1, w2_words, w2_sc
 
         gates = [keep.tile([P, T], F32, name="gate%d" % half, align_bytes=64) for half in range(2)]
         nc.sync.dma_start(gates[0][:], gT[0:P, :])
-
-        w2_w = keep.tile([P, 2 * M], U8, name="w2_w", align_bytes=64)
-        w2_sc = keep.tile([P, M], U8, name="w2_sc", align_bytes=64)
-        bias = keep.tile([P, 2], F32, name="bias")
-        nc.gpsimd.memset(w2_sc[:], 0)
-        nc.sync.dma_start(w2_w[:].bitcast(I32), w2_words[0].bitcast(I32))
-        for q in range(4):
-            nc.sync.dma_start(w2_sc[32 * q : 32 * q + 4, :].bitcast(I32), w2_scales[0, 4 * q : 4 * q + 4, :].bitcast(I32))
-        with nc.allow_non_contiguous_dma(reason="one bias value for each partition"):
-            nc.sync.dma_start(bias[:], b.rearrange("(h p) -> p h", p=P))
 
         nc.sync.dma_start(gates[1][:], gT[P : 2 * P, :])
 
@@ -75,6 +66,16 @@ def tile_list_tabgate_bias_kernel(tc, tab_words, tab_scales, w1, w2_words, w2_sc
             w1_bf[:].rearrange("p (t m j) -> p m t j", t=PACK, j=PACK),
             w1_raw[:].rearrange("p j (m t) -> p m t j", t=PACK),
         )
+        w2_w = reuse.tile([P, 2 * M], U8, name="w2_w", align_bytes=64, offset=0)
+        w2_sc = reuse.tile([P, M], U8, name="w2_sc", align_bytes=64, offset=2 * M)
+        bias = reuse.tile([P, 2], F32, name="bias", offset=4 * M)
+        nc.gpsimd.memset(w2_sc[:], 0)
+        nc.scalar.dma_start(w2_w[:].bitcast(I32), w2_words[0].bitcast(I32))
+        for q in range(4):
+            nc.scalar.dma_start(w2_sc[32 * q : 32 * q + 4, :].bitcast(I32), w2_scales[0, 4 * q : 4 * q + 4, :].bitcast(I32))
+        with nc.allow_non_contiguous_dma(reason="one bias value for each partition"):
+            nc.scalar.dma_start(bias[:], b.rearrange("(h p) -> p h", p=P))
+
         w1_q = keep.tile([P, R], U32, name="w1_q", align_bytes=64)
         w1_sc = keep.tile([P, R], U8, name="w1_sc", align_bytes=64)
         nc.vector.quantize_mx(out=w1_q[:].bitcast(FP8X4), scales=w1_sc[:], in_=w1_bf[:])
@@ -89,7 +90,7 @@ def tile_list_tabgate_bias_kernel(tc, tab_words, tab_scales, w1, w2_words, w2_sc
             v_w.append(vw)
 
         h_bf = [keep.tile([P, PACK * CHUNK], BF16, name="h_bf%d" % c, align_bytes=64) for c in range(S // CHUNK)]
-        h_q = [keep.tile([P, CHUNK], U32, name="h_q%d" % c, align_bytes=64) for c in range(S // CHUNK)]
+        h_q = {}
         h_sc = [keep.tile([P, CHUNK], U8, name="h_sc%d" % c, align_bytes=64) for c in range(S // CHUNK)]
         y_ps = {}
         y_sb = {}
@@ -114,7 +115,8 @@ def tile_list_tabgate_bias_kernel(tc, tab_words, tab_scales, w1, w2_words, w2_sc
             else:
                 nc.scalar.activation(dst, src, ACT.Relu)
 
-        def quantize_hidden(c):
+        def quantize_hidden(c, tag):
+            h_q[c] = keep.tile([P, CHUNK], U32, name="h_q%d" % c, tag=tag, align_bytes=64)
             nc.vector.quantize_mx(out=h_q[c][:].bitcast(FP8X4), scales=h_sc[c][:], in_=h_bf[c][:])
 
         def project(c, half):
@@ -131,49 +133,61 @@ def tile_list_tabgate_bias_kernel(tc, tab_words, tab_scales, w1, w2_words, w2_sc
             y_ps[c, half] = bank
 
         def add_bias(c, half):
-            y = keep.tile([P, CHUNK], F32, name="y%d_%d" % (c, half))
+            y = keep.tile([P, CHUNK], F32, name="y%d_%d" % (c, half), tag="y%d_%d" % (c, half))
             nc.scalar.activation(y[:], y_ps[c, half][:], ACT.Identity, bias=bias[:, half : half + 1])
             y_sb[c, half] = y
 
-        def gate(c, half, widths=(CHUNK,)):
+        def gate(c, half, tag, widths=(CHUNK,)):
             first = 0
             for width in widths:
-                res = keep.tile([P, width], F32, name="res%d_%d_%d" % (c, half, first))
+                res = keep.tile([P, width], F32, name="res%d_%d_%d" % (c, half, first), tag=tag if first == 0 else tag + "b")
                 token = c * CHUNK + first
                 nc.vector.tensor_tensor(res[:], gates[half][:].indirect(listed(token, width)), y_sb[c, half][:, first : first + width], ALU.mult)
                 nc.sync.dma_start(out[half * P : (half + 1) * P, token : token + width], res[:])
                 first += width
 
+        picked = {}
+
+        def pick_gates(c, half):
+            g = keep.tile([P, CHUNK], F32, name="picked%d_%d" % (c, half), tag="picked%d_%d" % (c, half), align_bytes=64)
+            nc.vector.tensor_copy(g[:], gates[half][:].indirect(listed(c * CHUNK, CHUNK)))
+            picked[c, half] = g
+
+        def gate_picked(c, half, tag):
+            res = keep.tile([P, CHUNK], F32, name="res%d_%d" % (c, half), tag=tag)
+            nc.vector.scalar_tensor_tensor(res[:], y_ps[c, half][:], bias[:, half : half + 1], picked[c, half][:], ALU.add, ALU.mult)
+            nc.sync.dma_start(out[half * P : (half + 1) * P, c * CHUNK : (c + 1) * CHUNK], res[:])
+
         hidden(0)
         hidden(1)
         hidden(2)
         hidden(3, on_vector=True)
-        quantize_hidden(0)
+        quantize_hidden(0, "h_q0")
+        pick_gates(0, 0)
         hidden(4)
         hidden(5)
         hidden(6)
-        hidden(7, on_vector=True)
+        hidden(7)
         project(0, 0)
-        quantize_hidden(1)
+        gate_picked(0, 0, "res00")
+        quantize_hidden(1, "picked0_0")
+        pick_gates(1, 0)
         hidden(8)
-        hidden(9, on_vector=True)
-        add_bias(0, 0)
+        hidden(9)
         hidden(10)
         hidden(11)
-        gate(0, 0)
         project(1, 0)
-        quantize_hidden(2)
-        add_bias(1, 0)
+        gate_picked(1, 0, "res10")
         project(0, 1)
         project(1, 1)
-        gate(1, 0)
+        quantize_hidden(2, "h_q2")
         add_bias(0, 1)
         add_bias(1, 1)
+        gate(0, 1, "res01")
         project(2, 0)
         project(2, 1)
-        gate(0, 1)
         add_bias(2, 0)
-        gate(1, 1)
         add_bias(2, 1)
-        gate(2, 0)
-        gate(2, 1, widths=(384, 128))
+        gate(1, 1, "res11")
+        gate(2, 0, "y1_1")
+        gate(2, 1, "res21", widths=(384, 128))

@@ -34,14 +34,14 @@ def tile_list_tabgate_bias_kernel(tc, tab_words, tab_scales, w1, w2_words, w2_sc
         offsets = keep.tile([P, S // LANES], U16, name="offsets")
         nc.sync.dma_start(offsets[:], offs)
 
-        w1_raw = reuse.tile([P, PACK, R], F32, name="w1_raw", offset=0)
+        w1_raw = keep.tile([P, PACK, R], F32, name="w1_raw")
         w1_rows = w1.rearrange("(p j) c -> p j c", j=PACK)
         nc.sync.dma_start(w1_raw[:, 0:2, :], w1_rows[:, 0:2, :])
 
         tab_sc = keep.tile([P, T], U8, name="tab_sc", align_bytes=64)
         nc.vector.memset(tab_sc[:].bitcast(I32), 0)
         for q in range(4):
-            nc.sync.dma_start(tab_sc[q:P:32, :].bitcast(I32), tab_scales[0, q:16:4, :].bitcast(I32))
+            nc.sync.dma_start(tab_sc[32 * q : 32 * q + 4, :].bitcast(I32), tab_scales[0, 4 * q : 4 * q + 4, :].bitcast(I32))
 
         nc.sync.dma_start(w1_raw[:, 2:4, :], w1_rows[:, 2:4, :])
 
@@ -61,24 +61,24 @@ def tile_list_tabgate_bias_kernel(tc, tab_words, tab_scales, w1, w2_words, w2_sc
         v_sc = keep.tile([P, S], U8, name="v_sc", align_bytes=64)
         nc.vector.tensor_copy(v_sc[:], tab_sc[:].indirect(offsets[:]))
 
-        w1_bf = keep.tile([P, PACK * R], BF16, name="w1_bf", align_bytes=64)
+        w1_bf = reuse.tile([P, PACK * R], BF16, name="w1_bf", align_bytes=64, offset=0)
         nc.scalar.copy(
             w1_bf[:].rearrange("p (t m j) -> p m t j", t=PACK, j=PACK),
             w1_raw[:].rearrange("p j (m t) -> p m t j", t=PACK),
         )
+        w1_q = keep.tile([P, R], U32, name="w1_q", align_bytes=64)
+        w1_sc = keep.tile([P, R], U8, name="w1_sc", align_bytes=64)
+        nc.vector.quantize_mx(out=w1_q[:].bitcast(FP8X4), scales=w1_sc[:], in_=w1_bf[:])
+
         w2_w = reuse.tile([P, 2 * M], U8, name="w2_w", align_bytes=64, offset=0)
         w2_sc = reuse.tile([P, M], U8, name="w2_sc", align_bytes=64, offset=2 * M)
         bias = reuse.tile([P, 2], F32, name="bias", offset=4 * M)
-        nc.gpsimd.memset(w2_sc[:], 0)
+        nc.vector.memset(w2_sc[:].bitcast(I32), 0)
         nc.scalar.dma_start(w2_w[:].bitcast(I32), w2_words[0].bitcast(I32))
         for q in range(4):
             nc.scalar.dma_start(w2_sc[32 * q : 32 * q + 4, :].bitcast(I32), w2_scales[0, 4 * q : 4 * q + 4, :].bitcast(I32))
         with nc.allow_non_contiguous_dma(reason="one bias value for each partition"):
             nc.scalar.dma_start(bias[:], b.rearrange("(h p) -> p h", p=P))
-
-        w1_q = keep.tile([P, R], U32, name="w1_q", align_bytes=64)
-        w1_sc = keep.tile([P, R], U8, name="w1_sc", align_bytes=64)
-        nc.vector.quantize_mx(out=w1_q[:].bitcast(FP8X4), scales=w1_sc[:], in_=w1_bf[:])
 
         def listed(first, count):
             return offsets[:, first // LANES : (first + count) // LANES]
@@ -89,7 +89,7 @@ def tile_list_tabgate_bias_kernel(tc, tab_words, tab_scales, w1, w2_words, w2_sc
             nc.vector.tensor_copy(vw[:], tab_w[:].indirect(listed(c * CHUNK, CHUNK)))
             v_w.append(vw)
 
-        h_bf = [keep.tile([P, PACK * CHUNK], BF16, name="h_bf%d" % c, align_bytes=64) for c in range(S // CHUNK)]
+        h_bf = [keep.tile([P, PACK * CHUNK], BF16, name="h_bf%d" % c, tag="h_bf%d" % c, align_bytes=64) for c in range(S // CHUNK)]
         h_q = {}
         h_sc = [keep.tile([P, CHUNK], U8, name="h_sc%d" % c, align_bytes=64) for c in range(S // CHUNK)]
         y_ps = {}
@@ -133,14 +133,14 @@ def tile_list_tabgate_bias_kernel(tc, tab_words, tab_scales, w1, w2_words, w2_sc
             y_ps[c, half] = bank
 
         def add_bias(c, half):
-            y = keep.tile([P, CHUNK], F32, name="y%d_%d" % (c, half), tag="y%d_%d" % (c, half))
+            y = keep.tile([P, CHUNK], F32, name="y%d_%d" % (c, half), tag="y%d_%d" % (c, half), align_bytes=64)
             nc.scalar.activation(y[:], y_ps[c, half][:], ACT.Identity, bias=bias[:, half : half + 1])
             y_sb[c, half] = y
 
         def gate(c, half, tag, widths=(CHUNK,)):
             first = 0
             for width in widths:
-                res = keep.tile([P, width], F32, name="res%d_%d_%d" % (c, half, first), tag=tag if first == 0 else tag + "b")
+                res = keep.tile([P, width], F32, name="res%d_%d_%d" % (c, half, first), tag=tag if first == 0 else tag + "b", align_bytes=64)
                 token = c * CHUNK + first
                 nc.vector.tensor_tensor(res[:], gates[half][:].indirect(listed(token, width)), y_sb[c, half][:, first : first + width], ALU.mult)
                 nc.sync.dma_start(out[half * P : (half + 1) * P, token : token + width], res[:])
@@ -163,24 +163,24 @@ def tile_list_tabgate_bias_kernel(tc, tab_words, tab_scales, w1, w2_words, w2_sc
         hidden(2)
         hidden(3, on_vector=True)
         quantize_hidden(0, "h_q0")
-        pick_gates(0, 0)
         hidden(4)
         hidden(5)
         hidden(6)
-        hidden(7)
+        hidden(7, on_vector=True)
         project(0, 0)
-        gate_picked(0, 0, "res00")
-        quantize_hidden(1, "picked0_0")
-        pick_gates(1, 0)
+        quantize_hidden(1, "h_q1")
         hidden(8)
+        add_bias(0, 0)
         hidden(9)
+        gate(0, 0, "h_bf1")
+        project(1, 0)
+        add_bias(1, 0)
         hidden(10)
         hidden(11)
-        project(1, 0)
-        gate_picked(1, 0, "res10")
+        gate(1, 0, "res10")
+        quantize_hidden(2, "h_q2")
         project(0, 1)
         project(1, 1)
-        quantize_hidden(2, "h_q2")
         add_bias(0, 1)
         add_bias(1, 1)
         gate(0, 1, "res01")

@@ -18,39 +18,57 @@ ALU = mybir.AluOpType
 
 P = 128
 PACK = 4
+QUADRANT = 32
+SCALE_ROWS = 4
+LANES = 16
 CHUNK = 512
 GROUP = 128
-LANES = 16
+BANKS = 4
+LAST_WIDTHS = (384, 128)
 
 
 def tile_list_tabgate_bias_kernel(tc, tab_words, tab_scales, w1, w2_words, w2_scales, gT, b, offs, out):
     nc = tc.nc
     with ExitStack() as ctx:
         keep = ctx.enter_context(tc.tile_pool(name="keep", bufs=1))
-        reuse = ctx.enter_context(tc.tile_pool(name="reuse", bufs=1))
-        psum_h = ctx.enter_context(tc.psum_pool(name="psum_h", bufs=4))
-        psum_y = ctx.enter_context(tc.psum_pool(name="psum_y", bufs=4))
+        psum_h = ctx.enter_context(tc.psum_pool(name="psum_h", bufs=BANKS))
+        psum_y = ctx.enter_context(tc.psum_pool(name="psum_y", bufs=BANKS))
 
         offsets = keep.tile([P, S // LANES], U16, name="offsets")
         nc.sync.dma_start(offsets[:], offs)
 
         w1_raw = keep.tile([P, PACK, R], F32, name="w1_raw")
         w1_rows = w1.rearrange("(p j) c -> p j c", j=PACK)
-        nc.sync.dma_start(w1_raw[:, 0:2, :], w1_rows[:, 0:2, :])
+        nc.sync.dma_start(w1_raw[:, 0 : PACK // 2, :], w1_rows[:, 0 : PACK // 2, :])
 
         tab_sc = keep.tile([P, T], U8, name="tab_sc", align_bytes=64)
         nc.vector.memset(tab_sc[:].bitcast(I32), 0)
-        for q in range(4):
-            nc.sync.dma_start(tab_sc[32 * q : 32 * q + 4, :].bitcast(I32), tab_scales[0, 4 * q : 4 * q + 4, :].bitcast(I32))
+        for quad in (0, 2, 1, 3):
+            nc.sync.dma_start(
+                tab_sc[QUADRANT * quad : QUADRANT * quad + SCALE_ROWS, :].bitcast(I32),
+                tab_scales[0, SCALE_ROWS * quad : SCALE_ROWS * (quad + 1), :].bitcast(I32),
+            )
 
-        nc.sync.dma_start(w1_raw[:, 2:4, :], w1_rows[:, 2:4, :])
+        nc.sync.dma_start(w1_raw[:, PACK // 2 : PACK, :], w1_rows[:, PACK // 2 : PACK, :])
 
         tab_w = keep.tile([P, T], U32, name="tab_w", align_bytes=64)
         nc.sync.dma_start(tab_w[:].bitcast(I32), tab_words[0].rearrange("p t i -> p (t i)").bitcast(I32))
 
-        gates = [keep.tile([P, T], F32, name="gate%d" % half, align_bytes=64) for half in range(2)]
-        nc.sync.dma_start(gates[0][:], gT[0:P, :])
+        gates = [keep.tile([P, T], F32, name="gate%d" % half, align_bytes=64) for half in range(M // P)]
+        w2_w = keep.tile([P, 2 * M], U8, name="w2_w", align_bytes=64)
+        w2_sc = keep.tile([P, M], U8, name="w2_sc", align_bytes=64)
+        bias = keep.tile([P, M // P], F32, name="bias")
+        nc.gpsimd.memset(w2_sc[:], 0)
+        nc.sync.dma_start(w2_w[:].bitcast(I32), w2_words[0].bitcast(I32))
+        for quad in range(P // QUADRANT):
+            nc.sync.dma_start(
+                w2_sc[QUADRANT * quad : QUADRANT * quad + SCALE_ROWS, :].bitcast(I32),
+                w2_scales[0, SCALE_ROWS * quad : SCALE_ROWS * (quad + 1), :].bitcast(I32),
+            )
+        with nc.allow_non_contiguous_dma(reason="one bias value for each partition"):
+            nc.sync.dma_start(bias[:], b.rearrange("(h p) -> p h", p=P))
 
+        nc.sync.dma_start(gates[0][:], gT[0:P, :])
         nc.sync.dma_start(gates[1][:], gT[P : 2 * P, :])
 
         warm_in = keep.tile([P, 1], F32, name="warm_in")
@@ -61,7 +79,7 @@ def tile_list_tabgate_bias_kernel(tc, tab_words, tab_scales, w1, w2_words, w2_sc
         v_sc = keep.tile([P, S], U8, name="v_sc", align_bytes=64)
         nc.vector.tensor_copy(v_sc[:], tab_sc[:].indirect(offsets[:]))
 
-        w1_bf = reuse.tile([P, PACK * R], BF16, name="w1_bf", align_bytes=64, offset=0)
+        w1_bf = keep.tile([P, PACK * R], BF16, name="w1_bf", align_bytes=64)
         nc.scalar.copy(
             w1_bf[:].rearrange("p (t m j) -> p m t j", t=PACK, j=PACK),
             w1_raw[:].rearrange("p j (m t) -> p m t j", t=PACK),
@@ -70,24 +88,14 @@ def tile_list_tabgate_bias_kernel(tc, tab_words, tab_scales, w1, w2_words, w2_sc
         w1_sc = keep.tile([P, R], U8, name="w1_sc", align_bytes=64)
         nc.vector.quantize_mx(out=w1_q[:].bitcast(FP8X4), scales=w1_sc[:], in_=w1_bf[:])
 
-        w2_w = reuse.tile([P, 2 * M], U8, name="w2_w", align_bytes=64, offset=0)
-        w2_sc = reuse.tile([P, M], U8, name="w2_sc", align_bytes=64, offset=2 * M)
-        bias = reuse.tile([P, 2], F32, name="bias", offset=4 * M)
-        nc.vector.memset(w2_sc[:].bitcast(I32), 0)
-        nc.scalar.dma_start(w2_w[:].bitcast(I32), w2_words[0].bitcast(I32))
-        for q in range(4):
-            nc.scalar.dma_start(w2_sc[32 * q : 32 * q + 4, :].bitcast(I32), w2_scales[0, 4 * q : 4 * q + 4, :].bitcast(I32))
-        with nc.allow_non_contiguous_dma(reason="one bias value for each partition"):
-            nc.scalar.dma_start(bias[:], b.rearrange("(h p) -> p h", p=P))
-
         def listed(first, count):
             return offsets[:, first // LANES : (first + count) // LANES]
 
         v_w = []
         for c in range(S // CHUNK):
-            vw = keep.tile([P, CHUNK], U32, name="v_w%d" % c, align_bytes=64)
-            nc.vector.tensor_copy(vw[:], tab_w[:].indirect(listed(c * CHUNK, CHUNK)))
-            v_w.append(vw)
+            words = keep.tile([P, CHUNK], U32, name="v_w%d" % c, align_bytes=64)
+            nc.vector.tensor_copy(words[:], tab_w[:].indirect(listed(c * CHUNK, CHUNK)))
+            v_w.append(words)
 
         h_bf = [keep.tile([P, PACK * CHUNK], BF16, name="h_bf%d" % c, tag="h_bf%d" % c, align_bytes=64) for c in range(S // CHUNK)]
         h_q = {}
@@ -146,18 +154,6 @@ def tile_list_tabgate_bias_kernel(tc, tab_words, tab_scales, w1, w2_words, w2_sc
                 nc.sync.dma_start(out[half * P : (half + 1) * P, token : token + width], res[:])
                 first += width
 
-        picked = {}
-
-        def pick_gates(c, half):
-            g = keep.tile([P, CHUNK], F32, name="picked%d_%d" % (c, half), tag="picked%d_%d" % (c, half), align_bytes=64)
-            nc.vector.tensor_copy(g[:], gates[half][:].indirect(listed(c * CHUNK, CHUNK)))
-            picked[c, half] = g
-
-        def gate_picked(c, half, tag):
-            res = keep.tile([P, CHUNK], F32, name="res%d_%d" % (c, half), tag=tag)
-            nc.vector.scalar_tensor_tensor(res[:], y_ps[c, half][:], bias[:, half : half + 1], picked[c, half][:], ALU.add, ALU.mult)
-            nc.sync.dma_start(out[half * P : (half + 1) * P, c * CHUNK : (c + 1) * CHUNK], res[:])
-
         hidden(0)
         hidden(1)
         hidden(2)
@@ -172,13 +168,13 @@ def tile_list_tabgate_bias_kernel(tc, tab_words, tab_scales, w1, w2_words, w2_sc
         hidden(8)
         add_bias(0, 0)
         hidden(9)
-        gate(0, 0, "h_bf1")
+        gate(0, 0, "res00")
         project(1, 0)
         add_bias(1, 0)
         hidden(10)
         hidden(11)
         gate(1, 0, "res10")
-        quantize_hidden(2, "h_q2")
+        quantize_hidden(2, "y1_0")
         project(0, 1)
         project(1, 1)
         add_bias(0, 1)
@@ -190,4 +186,4 @@ def tile_list_tabgate_bias_kernel(tc, tab_words, tab_scales, w1, w2_words, w2_sc
         add_bias(2, 1)
         gate(1, 1, "res11")
         gate(2, 0, "y1_1")
-        gate(2, 1, "res21", widths=(384, 128))
+        gate(2, 1, "res21", widths=LAST_WIDTHS)

@@ -20,6 +20,7 @@ P = 128
 PACK = 4
 QUADRANT = 32
 SCALE_ROWS = 4
+BLOCK = 8
 LANES = 16
 CHUNK = 512
 GROUP = 128
@@ -43,25 +44,31 @@ def tile_list_tabgate_bias_kernel(tc, tab_words, tab_scales, w1, w2_words, w2_sc
 
         tab_sc = keep.tile([P, T], U8, name="tab_sc", align_bytes=64)
         nc.vector.memset(tab_sc[:].bitcast(I32), 0)
-        for quad in (0, 2, 1, 3):
-            nc.sync.dma_start(
-                tab_sc[QUADRANT * quad : QUADRANT * quad + SCALE_ROWS, :].bitcast(I32),
-                tab_scales[0, SCALE_ROWS * quad : SCALE_ROWS * (quad + 1), :].bitcast(I32),
-            )
+        nc.sync.dma_start(tab_sc[0:P:BLOCK, :].bitcast(I32), tab_scales[0].bitcast(I32))
 
         nc.sync.dma_start(w1_raw[:, PACK // 2 : PACK, :], w1_rows[:, PACK // 2 : PACK, :])
 
         tab_w = keep.tile([P, T], U32, name="tab_w", align_bytes=64)
         nc.sync.dma_start(tab_w[:].bitcast(I32), tab_words[0].rearrange("p t i -> p (t i)").bitcast(I32))
 
+        picked_sc = keep.tile([P, S], U8, name="picked_sc", align_bytes=64)
+        nc.vector.tensor_copy(picked_sc[:], tab_sc[:].indirect(offsets[:]))
+        v_sc = keep.tile([P, S], U8, name="v_sc", align_bytes=64)
+        nc.gpsimd.memset(v_sc[:].bitcast(I32), 0)
+        for quad in (0, 2, 1, 3):
+            nc.sync.dma_start(
+                v_sc[QUADRANT * quad : QUADRANT * quad + SCALE_ROWS, :].bitcast(I32),
+                picked_sc[QUADRANT * quad : QUADRANT * (quad + 1) : BLOCK, :].bitcast(I32),
+            )
+
         gates = [keep.tile([P, T], F32, name="gate%d" % half, align_bytes=64) for half in range(M // P)]
         w2_w = keep.tile([P, 2 * M], U8, name="w2_w", align_bytes=64)
         w2_sc = keep.tile([P, M], U8, name="w2_sc", align_bytes=64)
         bias = keep.tile([P, M // P], F32, name="bias")
-        nc.gpsimd.memset(w2_sc[:], 0)
+        nc.gpsimd.memset(w2_sc[:].bitcast(I32), 0)
         nc.sync.dma_start(w2_w[:].bitcast(I32), w2_words[0].bitcast(I32))
         for quad in range(P // QUADRANT):
-            nc.sync.dma_start(
+            nc.gpsimd.dma_start(
                 w2_sc[QUADRANT * quad : QUADRANT * quad + SCALE_ROWS, :].bitcast(I32),
                 w2_scales[0, SCALE_ROWS * quad : SCALE_ROWS * (quad + 1), :].bitcast(I32),
             )
@@ -75,9 +82,6 @@ def tile_list_tabgate_bias_kernel(tc, tab_words, tab_scales, w1, w2_words, w2_sc
         warm_out = keep.tile([P, 1], F32, name="warm_out")
         nc.gpsimd.memset(warm_in[:], 0.0)
         nc.scalar.activation(warm_out[:], warm_in[:], ACT.Relu)
-
-        v_sc = keep.tile([P, S], U8, name="v_sc", align_bytes=64)
-        nc.vector.tensor_copy(v_sc[:], tab_sc[:].indirect(offsets[:]))
 
         w1_bf = keep.tile([P, PACK * R], BF16, name="w1_bf", align_bytes=64)
         nc.scalar.copy(

@@ -24,7 +24,6 @@ BLOCK = 8
 LANES = 16
 CHUNK = 512
 GROUP = 128
-BANKS = 4
 LAST_WIDTHS = (384, 128)
 
 
@@ -32,8 +31,7 @@ def tile_list_tabgate_bias_kernel(tc, tab_words, tab_scales, w1, w2_words, w2_sc
     nc = tc.nc
     with ExitStack() as ctx:
         keep = ctx.enter_context(tc.tile_pool(name="keep", bufs=1))
-        psum_h = ctx.enter_context(tc.psum_pool(name="psum_h", bufs=BANKS))
-        psum_y = ctx.enter_context(tc.psum_pool(name="psum_y", bufs=BANKS))
+        psum = ctx.enter_context(tc.psum_pool(name="psum", bufs=1))
 
         offsets = keep.tile([P, S // LANES], U16, name="offsets")
         nc.sync.dma_start(offsets[:], offs)
@@ -107,9 +105,9 @@ def tile_list_tabgate_bias_kernel(tc, tab_words, tab_scales, w1, w2_words, w2_sc
         y_ps = {}
         y_sb = {}
 
-        def hidden(group, on_vector=False):
+        def hidden(group, bank_no, on_vector=False):
             c, i = divmod(group, CHUNK // GROUP)
-            bank = psum_h.tile([P, PACK, GROUP], F32, name="h_bank")
+            bank = psum.tile([P, PACK, GROUP], F32, name="h_bank", tag="bank%d" % bank_no)
             for t in range(PACK):
                 nc.tensor.matmul_mx(
                     out=bank[:, t, :],
@@ -131,8 +129,8 @@ def tile_list_tabgate_bias_kernel(tc, tab_words, tab_scales, w1, w2_words, w2_sc
             h_q[c] = keep.tile([P, CHUNK], U32, name="h_q%d" % c, tag=tag, align_bytes=64)
             nc.vector.quantize_mx(out=h_q[c][:].bitcast(FP8X4), scales=h_sc[c][:], in_=h_bf[c][:])
 
-        def project(c, half):
-            bank = psum_y.tile([P, CHUNK], F32, name="y_bank")
+        def project(c, half, bank_no):
+            bank = psum.tile([P, CHUNK], F32, name="y_bank", tag="bank%d" % bank_no)
             nc.tensor.matmul_mx(
                 out=bank[:],
                 lhsT=w2_w[:, 2 * half * P : 2 * (half + 1) * P].bitcast(FP4X4),
@@ -158,36 +156,36 @@ def tile_list_tabgate_bias_kernel(tc, tab_words, tab_scales, w1, w2_words, w2_sc
                 nc.sync.dma_start(out[half * P : (half + 1) * P, token : token + width], res[:])
                 first += width
 
-        hidden(0)
-        hidden(1)
-        hidden(2)
-        hidden(3, on_vector=True)
+        hidden(0, 0)
+        hidden(1, 1)
+        hidden(2, 2, on_vector=True)
+        hidden(3, 3)
         quantize_hidden(0, "h_q0")
-        hidden(4)
-        hidden(5)
-        hidden(6)
-        hidden(7, on_vector=True)
-        project(0, 0)
+        hidden(4, 4)
+        hidden(5, 5)
+        hidden(6, 6, on_vector=True)
+        hidden(7, 7)
+        hidden(8, 0, on_vector=True)
+        project(0, 0, 1)
         quantize_hidden(1, "h_q1")
-        hidden(8)
         add_bias(0, 0)
-        hidden(9)
+        hidden(9, 2)
         gate(0, 0, "res00")
-        project(1, 0)
+        project(1, 0, 5)
         add_bias(1, 0)
-        hidden(10)
-        hidden(11)
+        hidden(10, 3)
+        hidden(11, 4)
         gate(1, 0, "res10")
-        quantize_hidden(2, "y1_0")
-        project(0, 1)
-        project(1, 1)
+        quantize_hidden(2, "y0_0")
+        project(0, 1, 3)
         add_bias(0, 1)
+        project(1, 1, 4)
         add_bias(1, 1)
         gate(0, 1, "res01")
-        project(2, 0)
-        project(2, 1)
+        project(2, 0, 6)
+        project(2, 1, 7)
         add_bias(2, 0)
         add_bias(2, 1)
         gate(1, 1, "res11")
-        gate(2, 0, "y1_1")
+        gate(2, 0, "y0_1")
         gate(2, 1, "res21", widths=LAST_WIDTHS)

@@ -31,16 +31,17 @@ def tile_list_tabgate_bias_kernel(tc, tab_words, tab_scales, w1, w2_words, w2_sc
     nc = tc.nc
     with ExitStack() as ctx:
         keep = ctx.enter_context(tc.tile_pool(name="keep", bufs=1))
+        late = ctx.enter_context(tc.tile_pool(name="late", bufs=1))
         psum = ctx.enter_context(tc.psum_pool(name="psum", bufs=1))
-
-        offsets = keep.tile([P, S // LANES], U16, name="offsets")
-        nc.sync.dma_start(offsets[:], offs)
 
         w1_raw = keep.tile([P, PACK, R], F32, name="w1_raw")
         w1_rows = w1.rearrange("(p j) c -> p j c", j=PACK)
         nc.sync.dma_start(w1_raw[:, 0 : PACK // 2, :], w1_rows[:, 0 : PACK // 2, :])
 
-        tab_sc = keep.tile([P, T], U8, name="tab_sc", align_bytes=64)
+        offsets = keep.tile([P, S // LANES], U16, name="offsets")
+        nc.sync.dma_start(offsets[:], offs)
+
+        tab_sc = late.tile([P, T], U8, name="tab_sc", align_bytes=64, offset=4 * T - 1024)
         nc.vector.memset(tab_sc[:].bitcast(I32), 0)
         nc.sync.dma_start(tab_sc[0:P:BLOCK, :].bitcast(I32), tab_scales[0].bitcast(I32))
 
@@ -59,10 +60,10 @@ def tile_list_tabgate_bias_kernel(tc, tab_words, tab_scales, w1, w2_words, w2_sc
                 picked_sc[QUADRANT * quad : QUADRANT * (quad + 1) : BLOCK, :].bitcast(I32),
             )
 
-        gates = [keep.tile([P, T], F32, name="gate%d" % half, align_bytes=64) for half in range(M // P)]
-        w2_w = keep.tile([P, 2 * M], U8, name="w2_w", align_bytes=64)
+        gates = [late.tile([P, T], F32, name="gate%d" % half, align_bytes=64, offset=(4 * T + 1024) * (1 - half)) for half in range(M // P)]
+        w2_w = late.tile([P, 2 * M], U8, name="w2_w", align_bytes=64, offset=4 * T)
         w2_sc = keep.tile([P, M], U8, name="w2_sc", align_bytes=64)
-        bias = keep.tile([P, M // P], F32, name="bias")
+        bias = late.tile([P, M // P], F32, name="bias", align_bytes=64, offset=4 * T + 2 * M)
         nc.gpsimd.memset(w2_sc[:].bitcast(I32), 0)
         nc.sync.dma_start(w2_w[:].bitcast(I32), w2_words[0].bitcast(I32))
         for quad in range(P // QUADRANT):
@@ -82,10 +83,11 @@ def tile_list_tabgate_bias_kernel(tc, tab_words, tab_scales, w1, w2_words, w2_sc
         nc.scalar.activation(warm_out[:], warm_in[:], ACT.Relu)
 
         w1_bf = keep.tile([P, PACK * R], BF16, name="w1_bf", align_bytes=64)
-        nc.scalar.copy(
-            w1_bf[:].rearrange("p (t m j) -> p m t j", t=PACK, j=PACK),
-            w1_raw[:].rearrange("p j (m t) -> p m t j", t=PACK),
-        )
+        for copy, places in ((nc.scalar.copy, slice(0, P // 2)), (nc.vector.tensor_copy, slice(P // 2, P))):
+            copy(
+                w1_bf[:].rearrange("p (t m j) -> p m t j", t=PACK, j=PACK)[:, places, :, :],
+                w1_raw[:].rearrange("p j (m t) -> p m t j", t=PACK)[:, places, :, :],
+            )
         w1_q = keep.tile([P, R], U32, name="w1_q", align_bytes=64)
         w1_sc = keep.tile([P, R], U8, name="w1_sc", align_bytes=64)
         nc.vector.quantize_mx(out=w1_q[:].bitcast(FP8X4), scales=w1_sc[:], in_=w1_bf[:])

@@ -53,7 +53,7 @@ def tile_list_tabgate_bias_kernel(tc, tab_words, tab_scales, w1, w2_words, w2_sc
         picked_sc = keep.tile([P, S], U8, name="picked_sc", align_bytes=64)
         nc.vector.tensor_copy(picked_sc[:], tab_sc[:].indirect(offsets[:]))
         v_sc = keep.tile([P, S], U8, name="v_sc", align_bytes=64)
-        nc.gpsimd.memset(v_sc[:].bitcast(I32), 0)
+        nc.vector.memset(v_sc[:].bitcast(I32), 0)
         for quad in (0, 2, 1, 3):
             nc.sync.dma_start(
                 v_sc[QUADRANT * quad : QUADRANT * quad + SCALE_ROWS, :].bitcast(I32),
@@ -64,7 +64,7 @@ def tile_list_tabgate_bias_kernel(tc, tab_words, tab_scales, w1, w2_words, w2_sc
         w2_w = late.tile([P, 2 * M], U8, name="w2_w", align_bytes=64, offset=4 * T)
         w2_sc = keep.tile([P, M], U8, name="w2_sc", align_bytes=64)
         bias = late.tile([P, M // P], F32, name="bias", align_bytes=64, offset=4 * T + 2 * M)
-        nc.gpsimd.memset(w2_sc[:].bitcast(I32), 0)
+        nc.vector.memset(w2_sc[:].bitcast(I32), 0)
         nc.sync.dma_start(w2_w[:].bitcast(I32), w2_words[0].bitcast(I32))
         for quad in range(P // QUADRANT):
             nc.gpsimd.dma_start(
@@ -79,7 +79,7 @@ def tile_list_tabgate_bias_kernel(tc, tab_words, tab_scales, w1, w2_words, w2_sc
 
         warm_in = keep.tile([P, 1], F32, name="warm_in")
         warm_out = keep.tile([P, 1], F32, name="warm_out")
-        nc.gpsimd.memset(warm_in[:], 0.0)
+        nc.vector.memset(warm_in[:], 0.0)
         nc.scalar.activation(warm_out[:], warm_in[:], ACT.Relu)
 
         w1_bf = keep.tile([P, PACK * R], BF16, name="w1_bf", align_bytes=64)

@@ -1,6 +1,7 @@
 from contextlib import ExitStack
 
 import concourse.mybir as mybir
+from concourse.masks import make_identity
 
 K, R, M, T, S = 512, 512, 256, 4096, 1536
 FLOPS = 2 * K * R * S + 2 * R * M * S
@@ -50,6 +51,10 @@ def tile_list_tabgate_bias_kernel(tc, tab_words, tab_scales, w1, w2_words, w2_sc
         tab_w = keep.tile([P, T], U32, name="tab_w", align_bytes=64)
         nc.sync.dma_start(tab_w[:].bitcast(I32), tab_words[0].rearrange("p t i -> p (t i)").bitcast(I32))
 
+        bias_rows = keep.tile([P, P], F32, name="bias_rows")
+        nc.vector.memset(bias_rows[:], 0.0)
+        nc.sync.dma_start(bias_rows[0 : M // P, :], b.rearrange("(h p) -> h p", p=P))
+
         picked_sc = keep.tile([P, S], U8, name="picked_sc", align_bytes=64)
         nc.vector.tensor_copy(picked_sc[:], tab_sc[:].indirect(offsets[:]))
         v_sc = keep.tile([P, S], U8, name="v_sc", align_bytes=64)
@@ -63,7 +68,12 @@ def tile_list_tabgate_bias_kernel(tc, tab_words, tab_scales, w1, w2_words, w2_sc
         gates = [late.tile([P, T], F32, name="gate%d" % half, align_bytes=64, offset=(4 * T + 1024) * (1 - half)) for half in range(M // P)]
         w2_w = late.tile([P, 2 * M], U8, name="w2_w", align_bytes=64, offset=4 * T)
         w2_sc = keep.tile([P, M], U8, name="w2_sc", align_bytes=64)
-        bias = late.tile([P, M // P], F32, name="bias", align_bytes=64, offset=4 * T + 2 * M)
+        bias = keep.tile([P, M // P], F32, name="bias")
+        identity = keep.tile([P, P], F32, name="identity")
+        make_identity(nc, identity[:])
+        bias_bank = psum.tile([P, P], F32, name="bias_bank", tag="bank7")
+        nc.tensor.transpose(bias_bank[:], bias_rows[:], identity[:])
+        nc.scalar.copy(bias[:], bias_bank[:, 0 : M // P])
         nc.vector.memset(w2_sc[:].bitcast(I32), 0)
         nc.sync.dma_start(w2_w[:].bitcast(I32), w2_words[0].bitcast(I32))
         for quad in range(P // QUADRANT):
@@ -71,8 +81,6 @@ def tile_list_tabgate_bias_kernel(tc, tab_words, tab_scales, w1, w2_words, w2_sc
                 w2_sc[QUADRANT * quad : QUADRANT * quad + SCALE_ROWS, :].bitcast(I32),
                 w2_scales[0, SCALE_ROWS * quad : SCALE_ROWS * (quad + 1), :].bitcast(I32),
             )
-        with nc.allow_non_contiguous_dma(reason="one bias value for each partition"):
-            nc.sync.dma_start(bias[:], b.rearrange("(h p) -> p h", p=P))
 
         nc.sync.dma_start(gates[0][:], gT[0:P, :])
         nc.sync.dma_start(gates[1][:], gT[P : 2 * P, :])

@@ -25,7 +25,11 @@ BLOCK = 8
 LANES = 16
 CHUNK = 512
 GROUP = 128
+BANKS = 8
 LAST_WIDTHS = (384, 128)
+VECTOR_GROUPS = (2, 6, 8)
+GATE_BYTES = 4 * T
+SHARED = 1024
 
 
 def tile_list_tabgate_bias_kernel(tc, tab_words, tab_scales, w1, w2_words, w2_scales, gT, b, offs, out):
@@ -42,7 +46,7 @@ def tile_list_tabgate_bias_kernel(tc, tab_words, tab_scales, w1, w2_words, w2_sc
         offsets = keep.tile([P, S // LANES], U16, name="offsets")
         nc.sync.dma_start(offsets[:], offs)
 
-        tab_sc = late.tile([P, T], U8, name="tab_sc", align_bytes=64, offset=4 * T - 1024)
+        tab_sc = late.tile([P, T], U8, name="tab_sc", align_bytes=64, offset=GATE_BYTES - SHARED)
         nc.vector.memset(tab_sc[:].bitcast(I32), 0)
         nc.sync.dma_start(tab_sc[0:P:BLOCK, :].bitcast(I32), tab_scales[0].bitcast(I32))
 
@@ -65,15 +69,18 @@ def tile_list_tabgate_bias_kernel(tc, tab_words, tab_scales, w1, w2_words, w2_sc
                 picked_sc[QUADRANT * quad : QUADRANT * (quad + 1) : BLOCK, :].bitcast(I32),
             )
 
-        gates = [late.tile([P, T], F32, name="gate%d" % half, align_bytes=64, offset=(4 * T + 1024) * (1 - half)) for half in range(M // P)]
-        w2_w = late.tile([P, 2 * M], U8, name="w2_w", align_bytes=64, offset=4 * T)
+        gate_offsets = (GATE_BYTES + SHARED, 0)
+        gates = [late.tile([P, T], F32, name="gate%d" % half, align_bytes=64, offset=gate_offsets[half]) for half in range(M // P)]
+        w2_w = late.tile([P, 2 * M], U8, name="w2_w", align_bytes=64, offset=GATE_BYTES)
         w2_sc = keep.tile([P, M], U8, name="w2_sc", align_bytes=64)
+
         bias = keep.tile([P, M // P], F32, name="bias")
         identity = keep.tile([P, P], F32, name="identity")
         make_identity(nc, identity[:])
-        bias_bank = psum.tile([P, P], F32, name="bias_bank", tag="bank7")
+        bias_bank = psum.tile([P, P], F32, name="bias_bank", tag="bank%d" % (BANKS - 1))
         nc.tensor.transpose(bias_bank[:], bias_rows[:], identity[:])
         nc.scalar.copy(bias[:], bias_bank[:, 0 : M // P])
+
         nc.vector.memset(w2_sc[:].bitcast(I32), 0)
         nc.sync.dma_start(w2_w[:].bitcast(I32), w2_words[0].bitcast(I32))
         for quad in range(P // QUADRANT):
@@ -84,11 +91,6 @@ def tile_list_tabgate_bias_kernel(tc, tab_words, tab_scales, w1, w2_words, w2_sc
 
         nc.sync.dma_start(gates[0][:], gT[0:P, :])
         nc.sync.dma_start(gates[1][:], gT[P : 2 * P, :])
-
-        warm_in = keep.tile([P, 1], F32, name="warm_in")
-        warm_out = keep.tile([P, 1], F32, name="warm_out")
-        nc.vector.memset(warm_in[:], 0.0)
-        nc.scalar.activation(warm_out[:], warm_in[:], ACT.Relu)
 
         w1_bf = keep.tile([P, PACK * R], BF16, name="w1_bf", align_bytes=64)
         for copy, places in ((nc.scalar.copy, slice(0, P // 2)), (nc.vector.tensor_copy, slice(P // 2, P))):
@@ -109,15 +111,23 @@ def tile_list_tabgate_bias_kernel(tc, tab_words, tab_scales, w1, w2_words, w2_sc
             nc.vector.tensor_copy(words[:], tab_w[:].indirect(listed(c * CHUNK, CHUNK)))
             v_w.append(words)
 
-        h_bf = [keep.tile([P, PACK * CHUNK], BF16, name="h_bf%d" % c, tag="h_bf%d" % c, align_bytes=64) for c in range(S // CHUNK)]
+        h_bf = [keep.tile([P, PACK * CHUNK], BF16, name="h_bf%d" % c, align_bytes=64) for c in range(S // CHUNK)]
         h_q = {}
         h_sc = [keep.tile([P, CHUNK], U8, name="h_sc%d" % c, align_bytes=64) for c in range(S // CHUNK)]
         y_ps = {}
         y_sb = {}
 
-        def hidden(group, bank_no, on_vector=False):
+        groups = S // GROUP
+        ahead = 2 * CHUNK // GROUP + 1
+        turns = [("h", g) for g in range(ahead)] + [("y", 0, 0)] + [("h", g) for g in range(ahead, groups)]
+        turns.extend([("y", 1, 0), ("y", 2, 0), ("y", 2, 1)])
+        bank_tag = {turn: "bank%d" % (n % BANKS) for n, turn in enumerate(turns)}
+        for c in range(2):
+            bank_tag["y", c, 1] = bank_tag["h", groups - 2 + c]
+
+        def hidden(group):
             c, i = divmod(group, CHUNK // GROUP)
-            bank = psum.tile([P, PACK, GROUP], F32, name="h_bank", tag="bank%d" % bank_no)
+            bank = psum.tile([P, PACK, GROUP], F32, name="h_bank", tag=bank_tag["h", group])
             for t in range(PACK):
                 nc.tensor.matmul_mx(
                     out=bank[:, t, :],
@@ -130,7 +140,7 @@ def tile_list_tabgate_bias_kernel(tc, tab_words, tab_scales, w1, w2_words, w2_sc
                 )
             dst = h_bf[c][:, i * GROUP * PACK : (i + 1) * GROUP * PACK].rearrange("p (n t) -> p n t", t=PACK)
             src = bank[:].rearrange("p t n -> p n t")
-            if on_vector:
+            if group in VECTOR_GROUPS:
                 nc.vector.tensor_scalar_max(dst, src, 0.0)
             else:
                 nc.scalar.activation(dst, src, ACT.Relu)
@@ -139,8 +149,8 @@ def tile_list_tabgate_bias_kernel(tc, tab_words, tab_scales, w1, w2_words, w2_sc
             h_q[c] = keep.tile([P, CHUNK], U32, name="h_q%d" % c, tag=tag, align_bytes=64)
             nc.vector.quantize_mx(out=h_q[c][:].bitcast(FP8X4), scales=h_sc[c][:], in_=h_bf[c][:])
 
-        def project(c, half, bank_no):
-            bank = psum.tile([P, CHUNK], F32, name="y_bank", tag="bank%d" % bank_no)
+        def project(c, half):
+            bank = psum.tile([P, CHUNK], F32, name="y_bank", tag=bank_tag["y", c, half])
             nc.tensor.matmul_mx(
                 out=bank[:],
                 lhsT=w2_w[:, 2 * half * P : 2 * (half + 1) * P].bitcast(FP4X4),
@@ -166,36 +176,31 @@ def tile_list_tabgate_bias_kernel(tc, tab_words, tab_scales, w1, w2_words, w2_sc
                 nc.sync.dma_start(out[half * P : (half + 1) * P, token : token + width], res[:])
                 first += width
 
-        hidden(0, 0)
-        hidden(1, 1)
-        hidden(2, 2, on_vector=True)
-        hidden(3, 3)
+        for group in range(CHUNK // GROUP):
+            hidden(group)
         quantize_hidden(0, "h_q0")
-        hidden(4, 4)
-        hidden(5, 5)
-        hidden(6, 6, on_vector=True)
-        hidden(7, 7)
-        hidden(8, 0, on_vector=True)
-        project(0, 0, 1)
+        for group in range(CHUNK // GROUP, ahead):
+            hidden(group)
+        project(0, 0)
         quantize_hidden(1, "h_q1")
         add_bias(0, 0)
-        hidden(9, 2)
+        hidden(ahead)
         gate(0, 0, "res00")
-        project(1, 0, 5)
+        project(1, 0)
         add_bias(1, 0)
-        hidden(10, 3)
-        hidden(11, 4)
+        for group in range(ahead + 1, groups):
+            hidden(group)
         gate(1, 0, "res10")
+
         quantize_hidden(2, "y0_0")
-        project(0, 1, 3)
-        add_bias(0, 1)
-        project(1, 1, 4)
-        add_bias(1, 1)
+        for c in range(2):
+            project(c, 1)
+            add_bias(c, 1)
         gate(0, 1, "res01")
-        project(2, 0, 6)
-        project(2, 1, 7)
-        add_bias(2, 0)
-        add_bias(2, 1)
+        for half in range(M // P):
+            project(2, half)
+        for half in range(M // P):
+            add_bias(2, half)
         gate(1, 1, "res11")
         gate(2, 0, "y0_1")
         gate(2, 1, "res21", widths=LAST_WIDTHS)

@@ -1,7 +1,6 @@
 from contextlib import ExitStack
 
 import concourse.mybir as mybir
-from concourse.masks import make_identity
 
 K, R, M, T, S = 512, 512, 256, 4096, 1536
 FLOPS = 2 * K * R * S + 2 * R * M * S
@@ -26,8 +25,9 @@ LANES = 16
 CHUNK = 512
 GROUP = 128
 BANKS = 8
-LAST_WIDTHS = (384, 128)
-VECTOR_GROUPS = (2, 6, 8)
+PAIR = 256
+AHEAD = 512
+SPLIT = 2560
 GATE_BYTES = 4 * T
 SHARED = 1024
 
@@ -46,8 +46,9 @@ def tile_list_tabgate_bias_kernel(tc, tab_words, tab_scales, w1, w2_words, w2_sc
         offsets = keep.tile([P, S // LANES], U16, name="offsets")
         nc.sync.dma_start(offsets[:], offs)
 
-        tab_sc = late.tile([P, T], U8, name="tab_sc", align_bytes=64, offset=GATE_BYTES - SHARED)
-        nc.vector.memset(tab_sc[:].bitcast(I32), 0)
+        tab_sc = keep.tile([P, T], U8, name="tab_sc", align_bytes=64)
+        nc.gpsimd.memset(tab_sc[:, 0 : T // 2].bitcast(I32), 0)
+        nc.vector.memset(tab_sc[:, T // 2 : T].bitcast(I32), 0)
         nc.sync.dma_start(tab_sc[0:P:BLOCK, :].bitcast(I32), tab_scales[0].bitcast(I32))
 
         nc.sync.dma_start(w1_raw[:, PACK // 2 : PACK, :], w1_rows[:, PACK // 2 : PACK, :])
@@ -55,11 +56,10 @@ def tile_list_tabgate_bias_kernel(tc, tab_words, tab_scales, w1, w2_words, w2_sc
         tab_w = keep.tile([P, T], U32, name="tab_w", align_bytes=64)
         nc.sync.dma_start(tab_w[:].bitcast(I32), tab_words[0].rearrange("p t i -> p (t i)").bitcast(I32))
 
-        bias_rows = keep.tile([P, P], F32, name="bias_rows")
-        nc.vector.memset(bias_rows[:], 0.0)
-        nc.sync.dma_start(bias_rows[0 : M // P, :], b.rearrange("(h p) -> h p", p=P))
+        gates = [late.tile([P, T], F32, name="gate%d" % half, align_bytes=64, offset=half * GATE_BYTES) for half in range(M // P)]
+        nc.sync.dma_start(gates[0][:, 0:AHEAD], gT[0:P, 0:AHEAD])
 
-        picked_sc = keep.tile([P, S], U8, name="picked_sc", align_bytes=64)
+        picked_sc = late.tile([P, S], U8, name="picked_sc", align_bytes=64, offset=GATE_BYTES)
         nc.vector.tensor_copy(picked_sc[:], tab_sc[:].indirect(offsets[:]))
         v_sc = keep.tile([P, S], U8, name="v_sc", align_bytes=64)
         nc.vector.memset(v_sc[:].bitcast(I32), 0)
@@ -69,19 +69,22 @@ def tile_list_tabgate_bias_kernel(tc, tab_words, tab_scales, w1, w2_words, w2_sc
                 picked_sc[QUADRANT * quad : QUADRANT * (quad + 1) : BLOCK, :].bitcast(I32),
             )
 
-        gate_offsets = (GATE_BYTES + SHARED, 0)
-        gates = [late.tile([P, T], F32, name="gate%d" % half, align_bytes=64, offset=gate_offsets[half]) for half in range(M // P)]
-        w2_w = late.tile([P, 2 * M], U8, name="w2_w", align_bytes=64, offset=GATE_BYTES)
+        w1_bf = keep.tile([P, PACK * R], BF16, name="w1_bf", align_bytes=64)
+        for rows in (slice(0, PACK // 2), slice(PACK // 2, PACK)):
+            nc.scalar.copy(
+                w1_bf[:].rearrange("p (t m j) -> p m t j", t=PACK, j=PACK)[:, :, :, rows],
+                w1_raw[:].rearrange("p j (m t) -> p m t j", t=PACK)[:, :, :, rows],
+            )
+
+        w2_w = keep.tile([P, 2 * M], U8, name="w2_w", align_bytes=64)
         w2_sc = keep.tile([P, M], U8, name="w2_sc", align_bytes=64)
 
         bias = keep.tile([P, M // P], F32, name="bias")
-        identity = keep.tile([P, P], F32, name="identity")
-        make_identity(nc, identity[:])
-        bias_bank = psum.tile([P, P], F32, name="bias_bank", tag="bank%d" % (BANKS - 1))
-        nc.tensor.transpose(bias_bank[:], bias_rows[:], identity[:])
-        nc.scalar.copy(bias[:], bias_bank[:, 0 : M // P])
+        with nc.allow_non_contiguous_dma(reason="one bias value for each partition and half"):
+            nc.gpsimd.dma_start(bias[:], b.rearrange("(h p) -> p h", p=P))
 
         nc.vector.memset(w2_sc[:].bitcast(I32), 0)
+        nc.sync.dma_start(gates[0][:, SPLIT:T], gT[0:P, SPLIT:T])
         nc.sync.dma_start(w2_w[:].bitcast(I32), w2_words[0].bitcast(I32))
         for quad in range(P // QUADRANT):
             nc.gpsimd.dma_start(
@@ -89,18 +92,13 @@ def tile_list_tabgate_bias_kernel(tc, tab_words, tab_scales, w1, w2_words, w2_sc
                 w2_scales[0, SCALE_ROWS * quad : SCALE_ROWS * (quad + 1), :].bitcast(I32),
             )
 
-        nc.sync.dma_start(gates[0][:], gT[0:P, :])
-        nc.sync.dma_start(gates[1][:], gT[P : 2 * P, :])
+        nc.scalar.dma_start(gates[0][:, AHEAD - 8 : SPLIT], gT[0:P, AHEAD - 8 : SPLIT])
+        nc.scalar.dma_start(gates[1][:], gT[P : 2 * P, :])
 
-        w1_bf = keep.tile([P, PACK * R], BF16, name="w1_bf", align_bytes=64)
-        for copy, places in ((nc.scalar.copy, slice(0, P // 2)), (nc.vector.tensor_copy, slice(P // 2, P))):
-            copy(
-                w1_bf[:].rearrange("p (t m j) -> p m t j", t=PACK, j=PACK)[:, places, :, :],
-                w1_raw[:].rearrange("p j (m t) -> p m t j", t=PACK)[:, places, :, :],
-            )
         w1_q = keep.tile([P, R], U32, name="w1_q", align_bytes=64)
         w1_sc = keep.tile([P, R], U8, name="w1_sc", align_bytes=64)
         nc.vector.quantize_mx(out=w1_q[:].bitcast(FP8X4), scales=w1_sc[:], in_=w1_bf[:])
+
 
         def listed(first, count):
             return offsets[:, first // LANES : (first + count) // LANES]
@@ -111,23 +109,17 @@ def tile_list_tabgate_bias_kernel(tc, tab_words, tab_scales, w1, w2_words, w2_sc
             nc.vector.tensor_copy(words[:], tab_w[:].indirect(listed(c * CHUNK, CHUNK)))
             v_w.append(words)
 
-        h_bf = [keep.tile([P, PACK * CHUNK], BF16, name="h_bf%d" % c, align_bytes=64) for c in range(S // CHUNK)]
-        h_q = {}
+        h_bf = [keep.tile([P, PACK * PAIR], BF16, name="h_bf%d" % n, tag="h_bf%d" % n, align_bytes=64) for n in range(S // PAIR)]
+        h_q = [keep.tile([P, CHUNK], U32, name="h_q%d" % c, align_bytes=64) for c in range(S // CHUNK)]
         h_sc = [keep.tile([P, CHUNK], U8, name="h_sc%d" % c, align_bytes=64) for c in range(S // CHUNK)]
+        results = [keep.tile([P, S], F32, name="res%d" % half, align_bytes=64) for half in range(M // P)]
+        h_ps = {}
         y_ps = {}
         y_sb = {}
 
-        groups = S // GROUP
-        ahead = 2 * CHUNK // GROUP + 1
-        turns = [("h", g) for g in range(ahead)] + [("y", 0, 0)] + [("h", g) for g in range(ahead, groups)]
-        turns.extend([("y", 1, 0), ("y", 2, 0), ("y", 2, 1)])
-        bank_tag = {turn: "bank%d" % (n % BANKS) for n, turn in enumerate(turns)}
-        for c in range(2):
-            bank_tag["y", c, 1] = bank_tag["h", groups - 2 + c]
-
-        def hidden(group):
+        def hidden(group, number):
             c, i = divmod(group, CHUNK // GROUP)
-            bank = psum.tile([P, PACK, GROUP], F32, name="h_bank", tag=bank_tag["h", group])
+            bank = psum.tile([P, PACK, GROUP], F32, name="h_bank", tag="bank%d" % number)
             for t in range(PACK):
                 nc.tensor.matmul_mx(
                     out=bank[:, t, :],
@@ -138,69 +130,117 @@ def tile_list_tabgate_bias_kernel(tc, tab_words, tab_scales, w1, w2_words, w2_sc
                     start=True,
                     stop=True,
                 )
-            dst = h_bf[c][:, i * GROUP * PACK : (i + 1) * GROUP * PACK].rearrange("p (n t) -> p n t", t=PACK)
-            src = bank[:].rearrange("p t n -> p n t")
-            if group in VECTOR_GROUPS:
+            h_ps[group] = bank
+
+        def relu(group, on_vector=False):
+            n, i = divmod(group, PAIR // GROUP)
+            dst = h_bf[n][:, i * GROUP * PACK : (i + 1) * GROUP * PACK].rearrange("p (n t) -> p n t", t=PACK)
+            src = h_ps[group][:].rearrange("p t n -> p n t")
+            if on_vector:
                 nc.vector.tensor_scalar_max(dst, src, 0.0)
             else:
                 nc.scalar.activation(dst, src, ACT.Relu)
 
-        def quantize_hidden(c, tag):
-            h_q[c] = keep.tile([P, CHUNK], U32, name="h_q%d" % c, tag=tag, align_bytes=64)
-            nc.vector.quantize_mx(out=h_q[c][:].bitcast(FP8X4), scales=h_sc[c][:], in_=h_bf[c][:])
+        def quantize(n):
+            c, i = divmod(n * PAIR, CHUNK)
+            nc.vector.quantize_mx(out=h_q[c][:, i : i + PAIR].bitcast(FP8X4), scales=h_sc[c][:, i : i + PAIR], in_=h_bf[n][:])
 
-        def project(c, half):
-            bank = psum.tile([P, CHUNK], F32, name="y_bank", tag=bank_tag["y", c, half])
+        def project(first, width, half, number):
+            c, i = divmod(first, CHUNK)
+            bank = psum.tile([P, CHUNK], F32, name="y_bank", tag="bank%d" % number)
             nc.tensor.matmul_mx(
-                out=bank[:],
+                out=bank[:, 0:width],
                 lhsT=w2_w[:, 2 * half * P : 2 * (half + 1) * P].bitcast(FP4X4),
                 lhsT_scale=w2_sc[:, half * P : (half + 1) * P],
-                rhs=h_q[c][:].bitcast(FP8X4),
-                rhs_scale=h_sc[c][:],
+                rhs=h_q[c][:, i : i + width].bitcast(FP8X4),
+                rhs_scale=h_sc[c][:, i : i + width],
                 start=True,
                 stop=True,
             )
-            y_ps[c, half] = bank
+            y_ps[first, half] = bank[:, 0:width]
 
-        def add_bias(c, half):
-            y = keep.tile([P, CHUNK], F32, name="y%d_%d" % (c, half), tag="y%d_%d" % (c, half), align_bytes=64)
-            nc.scalar.activation(y[:], y_ps[c, half][:], ACT.Identity, bias=bias[:, half : half + 1])
-            y_sb[c, half] = y
+        def add_bias(first, width, half):
+            y = keep.tile([P, width], F32, name="y%d_%d" % (first, half), align_bytes=64)
+            nc.scalar.activation(y[:], y_ps[first, half], ACT.Identity, bias=bias[:, half : half + 1])
+            y_sb[first, half] = y
 
-        def gate(c, half, tag, widths=(CHUNK,)):
-            first = 0
-            for width in widths:
-                res = keep.tile([P, width], F32, name="res%d_%d_%d" % (c, half, first), tag=tag if first == 0 else tag + "b", align_bytes=64)
-                token = c * CHUNK + first
-                nc.vector.tensor_tensor(res[:], gates[half][:].indirect(listed(token, width)), y_sb[c, half][:, first : first + width], ALU.mult)
-                nc.sync.dma_start(out[half * P : (half + 1) * P, token : token + width], res[:])
-                first += width
+        def store(first, width, half):
+            c, i = divmod(first, CHUNK)
+            nc.sync.dma_start(out[half * P : (half + 1) * P, first : first + width], results[half][:, first : first + width])
 
-        for group in range(CHUNK // GROUP):
-            hidden(group)
-        quantize_hidden(0, "h_q0")
-        for group in range(CHUNK // GROUP, ahead):
-            hidden(group)
-        project(0, 0)
-        quantize_hidden(1, "h_q1")
-        add_bias(0, 0)
-        hidden(ahead)
-        gate(0, 0, "res00")
-        project(1, 0)
-        add_bias(1, 0)
-        for group in range(ahead + 1, groups):
-            hidden(group)
-        gate(1, 0, "res10")
+        def gate(first, width, half, y_first=None):
+            c, i = divmod(first, CHUNK)
+            y_first = first if y_first is None else y_first
+            y = y_sb[y_first, half][:, first - y_first : first - y_first + width]
+            nc.vector.tensor_tensor(results[half][:, first : first + width], gates[half][:].indirect(listed(first, width)), y, ALU.mult)
 
-        quantize_hidden(2, "y0_0")
-        for c in range(2):
-            project(c, 1)
-            add_bias(c, 1)
-        gate(0, 1, "res01")
-        for half in range(M // P):
-            project(2, half)
-        for half in range(M // P):
-            add_bias(2, half)
-        gate(1, 1, "res11")
-        gate(2, 0, "y0_1")
-        gate(2, 1, "res21", widths=LAST_WIDTHS)
+        def pick(first, half, tag):
+            picked = keep.tile([P, CHUNK], F32, name="picked%d_%d" % (first, half), tag=tag, align_bytes=64)
+            nc.vector.tensor_copy(picked[:], gates[half][:].indirect(listed(first, CHUNK)))
+            return picked
+
+        def gate_picked(first, width, half, picked):
+            c, i = divmod(first, CHUNK)
+            nc.vector.scalar_tensor_tensor(results[half][:, first : first + width], y_ps[first, half], bias[:, half : half + 1], picked, ALU.add, ALU.mult)
+
+        hidden(0, 0)
+        hidden(1, 1)
+        hidden(2, 2)
+        hidden(3, 3)
+        hidden(4, 4)
+        hidden(5, 5)
+        hidden(6, 6)
+        hidden(7, 7)
+        relu(0)
+        hidden(8, 0)
+        relu(1)
+        hidden(9, 1)
+        relu(2)
+        relu(3, on_vector=True)
+        hidden(10, 3)
+        quantize(0)
+        quantize(1)
+        relu(4)
+        hidden(11, 4)
+        relu(5)
+        quantize(2)
+        project(512, 256, 0, 2)
+        picked = pick(0, 0, "h_bf0")
+        relu(6)
+        project(0, 512, 1, 5)
+        relu(7)
+        project(0, 512, 0, 7)
+        quantize(3)
+        project(768, 256, 0, 6)
+        gate_picked(0, 512, 0, picked[:])
+        relu(8)
+        add_bias(512, 256, 0)
+        gate(512, 256, 0, y_first=512)
+        relu(9)
+        quantize(4)
+        add_bias(768, 256, 0)
+        gate(768, 256, 0, y_first=768)
+        store(0, 1024, 0)
+        project(1024, 256, 0, 7)
+        project(512, 512, 1, 0)
+        add_bias(0, 512, 1)
+        gate(0, 512, 1, y_first=0)
+        store(0, 512, 1)
+        relu(10)
+        relu(11)
+        quantize(5)
+        project(1280, 256, 0, 1)
+        project(1024, 512, 1, 2)
+        add_bias(1024, 256, 0)
+        gate(1024, 256, 0, y_first=1024)
+        add_bias(512, 512, 1)
+        gate(512, 512, 1, y_first=512)
+        store(512, 512, 1)
+        add_bias(1280, 256, 0)
+        gate(1280, 256, 0, y_first=1280)
+        store(1024, 512, 0)
+        add_bias(1024, 512, 1)
+        gate(1024, 384, 1, y_first=1024)
+        store(1024, 384, 1)
+        gate(1408, 128, 1, y_first=1024)
+        store(1408, 128, 1)

@@ -1,6 +1,7 @@
 from contextlib import ExitStack
 
 import concourse.mybir as mybir
+from concourse.masks import make_identity
 
 K, R, M, T, S = 512, 512, 256, 4096, 1536
 FLOPS = 2 * K * R * S + 2 * R * M * S
@@ -53,6 +54,10 @@ def tile_list_tabgate_bias_kernel(tc, tab_words, tab_scales, w1, w2_words, w2_sc
 
         nc.sync.dma_start(w1_raw[:, PACK // 2 : PACK, :], w1_rows[:, PACK // 2 : PACK, :])
 
+        bias_rows = keep.tile([P, P], F32, name="bias_rows")
+        nc.vector.memset(bias_rows[:], 0.0)
+        nc.sync.dma_start(bias_rows[0 : M // P, :], b.rearrange("(h p) -> h p", p=P))
+
         tab_w = keep.tile([P, T], U32, name="tab_w", align_bytes=64)
         nc.sync.dma_start(tab_w[:].bitcast(I32), tab_words[0].rearrange("p t i -> p (t i)").bitcast(I32))
 
@@ -70,18 +75,21 @@ def tile_list_tabgate_bias_kernel(tc, tab_words, tab_scales, w1, w2_words, w2_sc
             )
 
         w1_bf = keep.tile([P, PACK * R], BF16, name="w1_bf", align_bytes=64)
-        for rows in (slice(0, PACK // 2), slice(PACK // 2, PACK)):
-            nc.scalar.copy(
-                w1_bf[:].rearrange("p (t m j) -> p m t j", t=PACK, j=PACK)[:, :, :, rows],
-                w1_raw[:].rearrange("p j (m t) -> p m t j", t=PACK)[:, :, :, rows],
+        for copy, places in ((nc.scalar.copy, slice(0, P // 2)), (nc.vector.tensor_copy, slice(P // 2, P))):
+            copy(
+                w1_bf[:].rearrange("p (t m j) -> p m t j", t=PACK, j=PACK)[:, places, :, :],
+                w1_raw[:].rearrange("p j (m t) -> p m t j", t=PACK)[:, places, :, :],
             )
 
         w2_w = keep.tile([P, 2 * M], U8, name="w2_w", align_bytes=64)
         w2_sc = keep.tile([P, M], U8, name="w2_sc", align_bytes=64)
 
         bias = keep.tile([P, M // P], F32, name="bias")
-        with nc.allow_non_contiguous_dma(reason="one bias value for each partition and half"):
-            nc.gpsimd.dma_start(bias[:], b.rearrange("(h p) -> p h", p=P))
+        identity = keep.tile([P, P], F32, name="identity")
+        make_identity(nc, identity[:])
+        bias_bank = psum.tile([P, P], F32, name="bias_bank", tag="bank%d" % (BANKS - 1))
+        nc.tensor.transpose(bias_bank[:], bias_rows[:], identity[:])
+        nc.scalar.copy(bias[:], bias_bank[:, 0 : M // P])
 
         nc.vector.memset(w2_sc[:].bitcast(I32), 0)
         nc.sync.dma_start(gates[0][:, SPLIT:T], gT[0:P, SPLIT:T])

@@ -28,7 +28,7 @@ GROUP = 128
 BANKS = 8
 PAIR = 256
 AHEAD = 512
-SPLIT = 2560
+SPLIT = 1536
 GATE_BYTES = 4 * T
 SHARED = 1024
 
@@ -113,7 +113,7 @@ def tile_list_tabgate_bias_kernel(tc, tab_words, tab_scales, w1, w2_words, w2_sc
 
         v_w = []
         for c in range(S // CHUNK):
-            words = keep.tile([P, CHUNK], U32, name="v_w%d" % c, align_bytes=64)
+            words = keep.tile([P, CHUNK], U32, name="v_w%d" % c, tag="v_w%d" % c, align_bytes=64)
             nc.vector.tensor_copy(words[:], tab_w[:].indirect(listed(c * CHUNK, CHUNK)))
             v_w.append(words)
 
@@ -198,30 +198,30 @@ def tile_list_tabgate_bias_kernel(tc, tab_words, tab_scales, w1, w2_words, w2_sc
         hidden(4, 4)
         hidden(5, 5)
         hidden(6, 6)
-        hidden(7, 7)
         relu(0)
-        hidden(8, 0)
         relu(1)
-        hidden(9, 1)
         relu(2)
+        hidden(7, 2)
         relu(3, on_vector=True)
-        hidden(10, 3)
         quantize(0)
         quantize(1)
+        picked = pick(0, 0, "v_w1")
         relu(4)
-        hidden(11, 4)
+        hidden(8, 4)
+        project(0, 512, 1, 3)
         relu(5)
+        project(0, 512, 0, 5)
         quantize(2)
-        project(512, 256, 0, 2)
-        picked = pick(0, 0, "h_bf0")
         relu(6)
-        project(0, 512, 1, 5)
-        relu(7)
-        project(0, 512, 0, 7)
-        quantize(3)
-        project(768, 256, 0, 6)
+        hidden(9, 6)
+        project(512, 256, 0, 0)
         gate_picked(0, 512, 0, picked[:])
+        relu(7)
+        hidden(10, 2)
+        quantize(3)
+        project(768, 256, 0, 1)
         relu(8)
+        hidden(11, 4)
         add_bias(512, 256, 0)
         gate(512, 256, 0, y_first=512)
         relu(9)
@@ -230,15 +230,15 @@ def tile_list_tabgate_bias_kernel(tc, tab_words, tab_scales, w1, w2_words, w2_sc
         gate(768, 256, 0, y_first=768)
         store(0, 1024, 0)
         project(1024, 256, 0, 7)
-        project(512, 512, 1, 0)
+        project(512, 512, 1, 5)
         add_bias(0, 512, 1)
         gate(0, 512, 1, y_first=0)
         store(0, 512, 1)
         relu(10)
         relu(11)
         quantize(5)
-        project(1280, 256, 0, 1)
-        project(1024, 512, 1, 2)
+        project(1280, 256, 0, 0)
+        project(1024, 512, 1, 1)
         add_bias(1024, 256, 0)
         gate(1024, 256, 0, y_first=1024)
         add_bias(512, 512, 1)

@@ -24,13 +24,15 @@ SCALE_ROWS = 4
 BLOCK = 8
 LANES = 16
 CHUNK = 512
-GROUP = 128
-BANKS = 8
 PAIR = 256
-AHEAD = 512
-SPLIT = 1536
+GROUP = 128
 GATE_BYTES = 4 * T
-SHARED = 1024
+AHEAD = 512
+LAST = 128
+VECTOR_GROUP = 3
+FIRST_GROUPS = 7
+H_BANKS = (2, 4, 6)
+Y_BANKS = (3, 5, 0, 1, 7)
 
 
 def tile_list_tabgate_bias_kernel(tc, tab_words, tab_scales, w1, w2_words, w2_scales, gT, b, offs, out):
@@ -83,16 +85,15 @@ def tile_list_tabgate_bias_kernel(tc, tab_words, tab_scales, w1, w2_words, w2_sc
 
         w2_w = keep.tile([P, 2 * M], U8, name="w2_w", align_bytes=64)
         w2_sc = keep.tile([P, M], U8, name="w2_sc", align_bytes=64)
-
         bias = keep.tile([P, M // P], F32, name="bias")
         identity = keep.tile([P, P], F32, name="identity")
         make_identity(nc, identity[:])
-        bias_bank = psum.tile([P, P], F32, name="bias_bank", tag="bank%d" % (BANKS - 1))
+        bias_bank = psum.tile([P, P], F32, name="bias_bank", tag="bank%d" % Y_BANKS[-1])
         nc.tensor.transpose(bias_bank[:], bias_rows[:], identity[:])
         nc.scalar.copy(bias[:], bias_bank[:, 0 : M // P])
 
         nc.vector.memset(w2_sc[:].bitcast(I32), 0)
-        nc.sync.dma_start(gates[0][:, SPLIT:T], gT[0:P, SPLIT:T])
+        nc.sync.dma_start(gates[0][:, AHEAD:T], gT[0:P, AHEAD:T])
         nc.sync.dma_start(w2_w[:].bitcast(I32), w2_words[0].bitcast(I32))
         for quad in range(P // QUADRANT):
             nc.gpsimd.dma_start(
@@ -100,16 +101,14 @@ def tile_list_tabgate_bias_kernel(tc, tab_words, tab_scales, w1, w2_words, w2_sc
                 w2_scales[0, SCALE_ROWS * quad : SCALE_ROWS * (quad + 1), :].bitcast(I32),
             )
 
-        nc.scalar.dma_start(gates[0][:, AHEAD - 8 : SPLIT], gT[0:P, AHEAD - 8 : SPLIT])
         nc.scalar.dma_start(gates[1][:], gT[P : 2 * P, :])
 
         w1_q = keep.tile([P, R], U32, name="w1_q", align_bytes=64)
         w1_sc = keep.tile([P, R], U8, name="w1_sc", align_bytes=64)
         nc.vector.quantize_mx(out=w1_q[:].bitcast(FP8X4), scales=w1_sc[:], in_=w1_bf[:])
 
-
-        def listed(first, count):
-            return offsets[:, first // LANES : (first + count) // LANES]
+        def listed(first, width):
+            return offsets[:, first // LANES : (first + width) // LANES]
 
         v_w = []
         for c in range(S // CHUNK):
@@ -117,7 +116,7 @@ def tile_list_tabgate_bias_kernel(tc, tab_words, tab_scales, w1, w2_words, w2_sc
             nc.vector.tensor_copy(words[:], tab_w[:].indirect(listed(c * CHUNK, CHUNK)))
             v_w.append(words)
 
-        h_bf = [keep.tile([P, PACK * PAIR], BF16, name="h_bf%d" % n, tag="h_bf%d" % n, align_bytes=64) for n in range(S // PAIR)]
+        h_bf = [keep.tile([P, PACK * PAIR], BF16, name="h_bf%d" % pair, align_bytes=64) for pair in range(S // PAIR)]
         h_q = [keep.tile([P, CHUNK], U32, name="h_q%d" % c, align_bytes=64) for c in range(S // CHUNK)]
         h_sc = [keep.tile([P, CHUNK], U8, name="h_sc%d" % c, align_bytes=64) for c in range(S // CHUNK)]
         results = [keep.tile([P, S], F32, name="res%d" % half, align_bytes=64) for half in range(M // P)]
@@ -125,37 +124,43 @@ def tile_list_tabgate_bias_kernel(tc, tab_words, tab_scales, w1, w2_words, w2_sc
         y_ps = {}
         y_sb = {}
 
-        def hidden(group, number):
-            c, i = divmod(group, CHUNK // GROUP)
-            bank = psum.tile([P, PACK, GROUP], F32, name="h_bank", tag="bank%d" % number)
+        def h_bank(group):
+            return group if group < FIRST_GROUPS else H_BANKS[(group - FIRST_GROUPS) % len(H_BANKS)]
+
+        def hidden(group):
+            c, i = divmod(group * GROUP, CHUNK)
+            bank = psum.tile([P, PACK, GROUP], F32, name="h_bank", tag="bank%d" % h_bank(group))
             for t in range(PACK):
                 nc.tensor.matmul_mx(
                     out=bank[:, t, :],
                     lhsT=w1_q[:, t * P : (t + 1) * P].bitcast(FP8X4),
                     lhsT_scale=w1_sc[:, t * P : (t + 1) * P],
-                    rhs=v_w[c][:, i * GROUP : (i + 1) * GROUP].bitcast(FP8X4),
+                    rhs=v_w[c][:, i : i + GROUP].bitcast(FP8X4),
                     rhs_scale=v_sc[:, group * GROUP : (group + 1) * GROUP],
                     start=True,
                     stop=True,
                 )
             h_ps[group] = bank
 
-        def relu(group, on_vector=False):
-            n, i = divmod(group, PAIR // GROUP)
-            dst = h_bf[n][:, i * GROUP * PACK : (i + 1) * GROUP * PACK].rearrange("p (n t) -> p n t", t=PACK)
+        def relu(group):
+            pair, i = divmod(group * GROUP, PAIR)
+            dst = h_bf[pair][:, PACK * i : PACK * (i + GROUP)].rearrange("p (n t) -> p n t", t=PACK)
             src = h_ps[group][:].rearrange("p t n -> p n t")
-            if on_vector:
+            if group == VECTOR_GROUP:
                 nc.vector.tensor_scalar_max(dst, src, 0.0)
             else:
                 nc.scalar.activation(dst, src, ACT.Relu)
+            following = len(h_ps)
+            if following < S // GROUP and h_bank(following) == h_bank(group):
+                hidden(following)
 
-        def quantize(n):
-            c, i = divmod(n * PAIR, CHUNK)
-            nc.vector.quantize_mx(out=h_q[c][:, i : i + PAIR].bitcast(FP8X4), scales=h_sc[c][:, i : i + PAIR], in_=h_bf[n][:])
+        def quantize(pair):
+            c, i = divmod(pair * PAIR, CHUNK)
+            nc.vector.quantize_mx(out=h_q[c][:, i : i + PAIR].bitcast(FP8X4), scales=h_sc[c][:, i : i + PAIR], in_=h_bf[pair][:])
 
-        def project(first, width, half, number):
+        def project(first, width, half):
             c, i = divmod(first, CHUNK)
-            bank = psum.tile([P, CHUNK], F32, name="y_bank", tag="bank%d" % number)
+            bank = psum.tile([P, CHUNK], F32, name="y_bank", tag="bank%d" % Y_BANKS[len(y_ps) % len(Y_BANKS)])
             nc.tensor.matmul_mx(
                 out=bank[:, 0:width],
                 lhsT=w2_w[:, 2 * half * P : 2 * (half + 1) * P].bitcast(FP4X4),
@@ -172,83 +177,67 @@ def tile_list_tabgate_bias_kernel(tc, tab_words, tab_scales, w1, w2_words, w2_sc
             nc.scalar.activation(y[:], y_ps[first, half], ACT.Identity, bias=bias[:, half : half + 1])
             y_sb[first, half] = y
 
+        def gate(first, width, half, skip=0):
+            token = first + skip
+            nc.vector.tensor_tensor(
+                results[half][:, token : token + width],
+                gates[half][:].indirect(listed(token, width)),
+                y_sb[first, half][:, skip : skip + width],
+                ALU.mult,
+            )
+
         def store(first, width, half):
-            c, i = divmod(first, CHUNK)
             nc.sync.dma_start(out[half * P : (half + 1) * P, first : first + width], results[half][:, first : first + width])
 
-        def gate(first, width, half, y_first=None):
-            c, i = divmod(first, CHUNK)
-            y_first = first if y_first is None else y_first
-            y = y_sb[y_first, half][:, first - y_first : first - y_first + width]
-            nc.vector.tensor_tensor(results[half][:, first : first + width], gates[half][:].indirect(listed(first, width)), y, ALU.mult)
-
-        def pick(first, half, tag):
-            picked = keep.tile([P, CHUNK], F32, name="picked%d_%d" % (first, half), tag=tag, align_bytes=64)
-            nc.vector.tensor_copy(picked[:], gates[half][:].indirect(listed(first, CHUNK)))
-            return picked
-
-        def gate_picked(first, width, half, picked):
-            c, i = divmod(first, CHUNK)
-            nc.vector.scalar_tensor_tensor(results[half][:, first : first + width], y_ps[first, half], bias[:, half : half + 1], picked, ALU.add, ALU.mult)
-
-        hidden(0, 0)
-        hidden(1, 1)
-        hidden(2, 2)
-        hidden(3, 3)
-        hidden(4, 4)
-        hidden(5, 5)
-        hidden(6, 6)
-        relu(0)
-        relu(1)
-        relu(2)
-        hidden(7, 2)
-        relu(3, on_vector=True)
+        for group in range(FIRST_GROUPS):
+            hidden(group)
+        for group in range(CHUNK // GROUP):
+            relu(group)
         quantize(0)
         quantize(1)
-        picked = pick(0, 0, "v_w1")
+
+        picked = keep.tile([P, CHUNK], F32, name="picked", tag="v_w1", align_bytes=64)
+        nc.vector.tensor_copy(picked[:], gates[0][:].indirect(listed(0, CHUNK)))
         relu(4)
-        hidden(8, 4)
-        project(0, 512, 1, 3)
+        project(0, CHUNK, 1)
         relu(5)
-        project(0, 512, 0, 5)
+        project(0, CHUNK, 0)
         quantize(2)
         relu(6)
-        hidden(9, 6)
-        project(512, 256, 0, 0)
-        gate_picked(0, 512, 0, picked[:])
+        project(2 * PAIR, PAIR, 0)
+        nc.vector.scalar_tensor_tensor(results[0][:, 0:CHUNK], y_ps[0, 0], bias[:, 0:1], picked[:], ALU.add, ALU.mult)
         relu(7)
-        hidden(10, 2)
         quantize(3)
-        project(768, 256, 0, 1)
+        project(3 * PAIR, PAIR, 0)
+
         relu(8)
-        hidden(11, 4)
-        add_bias(512, 256, 0)
-        gate(512, 256, 0, y_first=512)
+        add_bias(2 * PAIR, PAIR, 0)
+        gate(2 * PAIR, PAIR, 0)
         relu(9)
         quantize(4)
-        add_bias(768, 256, 0)
-        gate(768, 256, 0, y_first=768)
-        store(0, 1024, 0)
-        project(1024, 256, 0, 7)
-        project(512, 512, 1, 5)
-        add_bias(0, 512, 1)
-        gate(0, 512, 1, y_first=0)
-        store(0, 512, 1)
+        add_bias(3 * PAIR, PAIR, 0)
+        gate(3 * PAIR, PAIR, 0)
+        store(0, 2 * CHUNK, 0)
+        project(4 * PAIR, PAIR, 0)
+
+        add_bias(0, CHUNK, 1)
+        project(CHUNK, CHUNK, 1)
+        gate(0, CHUNK, 1)
+        store(0, CHUNK, 1)
         relu(10)
         relu(11)
         quantize(5)
-        project(1280, 256, 0, 0)
-        project(1024, 512, 1, 1)
-        add_bias(1024, 256, 0)
-        gate(1024, 256, 0, y_first=1024)
-        add_bias(512, 512, 1)
-        gate(512, 512, 1, y_first=512)
-        store(512, 512, 1)
-        add_bias(1280, 256, 0)
-        gate(1280, 256, 0, y_first=1280)
-        store(1024, 512, 0)
-        add_bias(1024, 512, 1)
-        gate(1024, 384, 1, y_first=1024)
-        store(1024, 384, 1)
-        gate(1408, 128, 1, y_first=1024)
-        store(1408, 128, 1)
+        project(5 * PAIR, PAIR, 0)
+        project(2 * CHUNK, CHUNK, 1)
+        add_bias(4 * PAIR, PAIR, 0)
+        gate(4 * PAIR, PAIR, 0)
+        add_bias(CHUNK, CHUNK, 1)
+        gate(CHUNK, CHUNK, 1)
+        store(CHUNK, CHUNK, 1)
+        add_bias(5 * PAIR, PAIR, 0)
+        gate(5 * PAIR, PAIR, 0)
+        store(2 * CHUNK, CHUNK, 0)
+        add_bias(2 * CHUNK, CHUNK, 1)
+        for skip, width in ((0, CHUNK - LAST), (CHUNK - LAST, LAST)):
+            gate(2 * CHUNK, width, 1, skip)
+            store(2 * CHUNK + skip, width, 1)

@@ -29,6 +29,7 @@ GROUP = 128
 GATE_BYTES = 4 * T
 AHEAD = 512
 LAST = 128
+WARM_UP = (512, 256, 128)
 VECTOR_GROUP = 3
 FIRST_GROUPS = 7
 H_BANKS = (2, 4, 6)
@@ -106,6 +107,18 @@ def tile_list_tabgate_bias_kernel(tc, tab_words, tab_scales, w1, w2_words, w2_sc
         w1_q = keep.tile([P, R], U32, name="w1_q", align_bytes=64)
         w1_sc = keep.tile([P, R], U8, name="w1_sc", align_bytes=64)
         nc.vector.quantize_mx(out=w1_q[:].bitcast(FP8X4), scales=w1_sc[:], in_=w1_bf[:])
+
+        warm = psum.tile([P, CHUNK], F32, name="warm", tag="bank%d" % (FIRST_GROUPS - 1))
+        for width in WARM_UP:
+            nc.tensor.matmul_mx(
+                out=warm[:, 0:width],
+                lhsT=w1_q[:, 0:P].bitcast(FP8X4),
+                lhsT_scale=w1_sc[:, 0:P],
+                rhs=w1_q[:, 0:width].bitcast(FP8X4),
+                rhs_scale=w1_sc[:, 0:width],
+                start=True,
+                stop=True,
+            )
 
         def listed(first, width):
             return offsets[:, first // LANES : (first + width) // LANES]

@@ -21,7 +21,7 @@ P = 128
 PACK = 4
 QUADRANT = 32
 SCALE_ROWS = 4
-BLOCK = 8
+SPREAD_FIRST, SPREAD = 32, 4
 LANES = 16
 CHUNK = 512
 PAIR = 256
@@ -51,9 +51,8 @@ def tile_list_tabgate_bias_kernel(tc, tab_words, tab_scales, w1, w2_words, w2_sc
         nc.sync.dma_start(offsets[:], offs)
 
         tab_sc = keep.tile([P, T], U8, name="tab_sc", align_bytes=64)
-        nc.gpsimd.memset(tab_sc[:, 0 : T // 2].bitcast(I32), 0)
-        nc.vector.memset(tab_sc[:, T // 2 : T].bitcast(I32), 0)
-        nc.sync.dma_start(tab_sc[0:P:BLOCK, :].bitcast(I32), tab_scales[0].bitcast(I32))
+        nc.vector.memset(tab_sc[:].bitcast(I32), 0)
+        nc.sync.dma_start(tab_sc[SPREAD_FIRST : SPREAD_FIRST + 16 * SPREAD : SPREAD, :].bitcast(I32), tab_scales[0].bitcast(I32))
 
         nc.sync.dma_start(w1_raw[:, PACK // 2 : PACK, :], w1_rows[:, PACK // 2 : PACK, :])
 
@@ -74,7 +73,7 @@ def tile_list_tabgate_bias_kernel(tc, tab_words, tab_scales, w1, w2_words, w2_sc
         for quad in (0, 2, 1, 3):
             nc.sync.dma_start(
                 v_sc[QUADRANT * quad : QUADRANT * quad + SCALE_ROWS, :].bitcast(I32),
-                picked_sc[QUADRANT * quad : QUADRANT * (quad + 1) : BLOCK, :].bitcast(I32),
+                picked_sc[SPREAD_FIRST + SCALE_ROWS * SPREAD * quad : SPREAD_FIRST + SCALE_ROWS * SPREAD * (quad + 1) : SPREAD, :].bitcast(I32),
             )
 
         w1_bf = keep.tile([P, PACK * R], BF16, name="w1_bf", align_bytes=64)

@@ -229,7 +229,6 @@ def tile_list_tabgate_bias_kernel(tc, tab_words, tab_scales, w1, w2_words, w2_sc
         quantize(4)
         add_bias(3 * PAIR, PAIR, 0)
         gate(3 * PAIR, PAIR, 0)
-        store(0, 2 * CHUNK, 0)
         project(4 * PAIR, PAIR, 0)
 
         add_bias(0, CHUNK, 1)
@@ -243,12 +242,13 @@ def tile_list_tabgate_bias_kernel(tc, tab_words, tab_scales, w1, w2_words, w2_sc
         project(2 * CHUNK, CHUNK, 1)
         add_bias(4 * PAIR, PAIR, 0)
         gate(4 * PAIR, PAIR, 0)
+        store(0, 5 * PAIR, 0)
         add_bias(CHUNK, CHUNK, 1)
         gate(CHUNK, CHUNK, 1)
         store(CHUNK, CHUNK, 1)
         add_bias(5 * PAIR, PAIR, 0)
         gate(5 * PAIR, PAIR, 0)
-        store(2 * CHUNK, CHUNK, 0)
+        store(5 * PAIR, PAIR, 0)
         add_bias(2 * CHUNK, CHUNK, 1)
         for skip, width in ((0, CHUNK - LAST), (CHUNK - LAST, LAST)):
             gate(2 * CHUNK, width, 1, skip)

@@ -1,7 +1,6 @@
 from contextlib import ExitStack
 
 import concourse.mybir as mybir
-from concourse.masks import make_identity
 
 K, R, M, T, S = 512, 512, 256, 4096, 1536
 FLOPS = 2 * K * R * S + 2 * R * M * S
@@ -22,6 +21,7 @@ PACK = 4
 QUADRANT = 32
 SCALE_ROWS = 4
 SPREAD_FIRST, SPREAD = 32, 4
+PLANE = 4
 LANES = 16
 CHUNK = 512
 PAIR = 256
@@ -56,9 +56,13 @@ def tile_list_tabgate_bias_kernel(tc, tab_words, tab_scales, w1, w2_words, w2_sc
 
         nc.sync.dma_start(w1_raw[:, PACK // 2 : PACK, :], w1_rows[:, PACK // 2 : PACK, :])
 
-        bias_rows = keep.tile([P, P], F32, name="bias_rows")
+        bias_rows = keep.tile([P, P], F32, name="bias_rows", align_bytes=64)
         nc.vector.memset(bias_rows[:], 0.0)
-        nc.sync.dma_start(bias_rows[0 : M // P, :], b.rearrange("(h p) -> h p", p=P))
+
+        nc.sync.dma_start(
+            bias_rows[0:P:QUADRANT, 0 : M // P * QUADRANT].rearrange("q (h i) -> q h i", i=QUADRANT),
+            b.rearrange("(h q i) -> q h i", h=M // P, i=QUADRANT),
+        )
 
         tab_w = keep.tile([P, T], U32, name="tab_w", align_bytes=64)
         nc.sync.dma_start(tab_w[:].bitcast(I32), tab_words[0].rearrange("p t i -> p (t i)").bitcast(I32))
@@ -72,7 +76,7 @@ def tile_list_tabgate_bias_kernel(tc, tab_words, tab_scales, w1, w2_words, w2_sc
         nc.vector.memset(v_sc[:].bitcast(I32), 0)
         for quad in (0, 2, 1, 3):
             nc.sync.dma_start(
-                v_sc[QUADRANT * quad : QUADRANT * quad + SCALE_ROWS, :].bitcast(I32),
+                v_sc[QUADRANT * quad + PLANE : QUADRANT * quad + PLANE + SCALE_ROWS, :].bitcast(I32),
                 picked_sc[SPREAD_FIRST + SCALE_ROWS * SPREAD * quad : SPREAD_FIRST + SCALE_ROWS * SPREAD * (quad + 1) : SPREAD, :].bitcast(I32),
             )
 
@@ -85,12 +89,8 @@ def tile_list_tabgate_bias_kernel(tc, tab_words, tab_scales, w1, w2_words, w2_sc
 
         w2_w = keep.tile([P, 2 * M], U8, name="w2_w", align_bytes=64)
         w2_sc = keep.tile([P, M], U8, name="w2_sc", align_bytes=64)
-        bias = keep.tile([P, M // P], F32, name="bias")
-        identity = keep.tile([P, P], F32, name="identity")
-        make_identity(nc, identity[:])
-        bias_bank = psum.tile([P, P], F32, name="bias_bank", tag="bank%d" % Y_BANKS[-1])
-        nc.tensor.transpose(bias_bank[:], bias_rows[:], identity[:])
-        nc.scalar.copy(bias[:], bias_bank[:, 0 : M // P])
+        bias = keep.tile([P, P], F32, name="bias", align_bytes=64)
+        nc.vector.transpose(bias[:], bias_rows[:])
 
         nc.vector.memset(w2_sc[:].bitcast(I32), 0)
         nc.sync.dma_start(gates[0][:, AHEAD:T], gT[0:P, AHEAD:T])
@@ -148,7 +148,7 @@ def tile_list_tabgate_bias_kernel(tc, tab_words, tab_scales, w1, w2_words, w2_sc
                     lhsT=w1_q[:, t * P : (t + 1) * P].bitcast(FP8X4),
                     lhsT_scale=w1_sc[:, t * P : (t + 1) * P],
                     rhs=v_w[c][:, i : i + GROUP].bitcast(FP8X4),
-                    rhs_scale=v_sc[:, group * GROUP : (group + 1) * GROUP],
+                    rhs_scale=v_sc[PLANE:P, group * GROUP : (group + 1) * GROUP],
                     start=True,
                     stop=True,
                 )
@@ -186,7 +186,7 @@ def tile_list_tabgate_bias_kernel(tc, tab_words, tab_scales, w1, w2_words, w2_sc
 
         def add_bias(first, width, half):
             y = keep.tile([P, width], F32, name="y%d_%d" % (first, half), align_bytes=64)
-            nc.scalar.activation(y[:], y_ps[first, half], ACT.Identity, bias=bias[:, half : half + 1])
+            nc.scalar.activation(y[:], y_ps[first, half], ACT.Identity, bias=bias[:, QUADRANT * half : QUADRANT * half + 1])
             y_sb[first, half] = y
 
         def gate(first, width, half, skip=0):
@@ -229,6 +229,7 @@ def tile_list_tabgate_bias_kernel(tc, tab_words, tab_scales, w1, w2_words, w2_sc
         quantize(4)
         add_bias(3 * PAIR, PAIR, 0)
         gate(3 * PAIR, PAIR, 0)
+        store(0, 4 * PAIR, 0)
         project(4 * PAIR, PAIR, 0)
 
         add_bias(0, CHUNK, 1)
@@ -242,7 +243,7 @@ def tile_list_tabgate_bias_kernel(tc, tab_words, tab_scales, w1, w2_words, w2_sc
         project(2 * CHUNK, CHUNK, 1)
         add_bias(4 * PAIR, PAIR, 0)
         gate(4 * PAIR, PAIR, 0)
-        store(0, 5 * PAIR, 0)
+        store(4 * PAIR, PAIR, 0)
         add_bias(CHUNK, CHUNK, 1)
         gate(CHUNK, CHUNK, 1)
         store(CHUNK, CHUNK, 1)

@@ -28,7 +28,7 @@ PAIR = 256
 GROUP = 128
 GATE_BYTES = 4 * T
 AHEAD = 512
-LAST = 128
+LAST = 192
 WARM_UP = (512, 256, 128)
 VECTOR_GROUP = 3
 FIRST_GROUPS = 7

@@ -27,7 +27,8 @@ CHUNK = 512
 PAIR = 256
 GROUP = 128
 GATE_BYTES = 4 * T
-AHEAD = 512
+FIRST_W1 = 768
+AHEAD = 320
 LAST = 192
 WARM_UP = (512, 256, 128)
 VECTOR_GROUP = 3
@@ -44,8 +45,9 @@ def tile_list_tabgate_bias_kernel(tc, tab_words, tab_scales, w1, w2_words, w2_sc
         psum = ctx.enter_context(tc.psum_pool(name="psum", bufs=1))
 
         w1_raw = keep.tile([P, PACK, R], F32, name="w1_raw")
-        w1_rows = w1.rearrange("(p j) c -> p j c", j=PACK)
-        nc.sync.dma_start(w1_raw[:, 0 : PACK // 2, :], w1_rows[:, 0 : PACK // 2, :])
+        w1_rows = w1.rearrange("(p j) c -> p (j c)", j=PACK)
+        w1_flat = w1_raw[:].rearrange("p j c -> p (j c)")
+        nc.sync.dma_start(w1_flat[:, 0:FIRST_W1], w1_rows[:, 0:FIRST_W1])
 
         offsets = keep.tile([P, S // LANES], U16, name="offsets")
         nc.sync.dma_start(offsets[:], offs)
@@ -54,7 +56,7 @@ def tile_list_tabgate_bias_kernel(tc, tab_words, tab_scales, w1, w2_words, w2_sc
         nc.vector.memset(tab_sc[:].bitcast(I32), 0)
         nc.sync.dma_start(tab_sc[SPREAD_FIRST : SPREAD_FIRST + 16 * SPREAD : SPREAD, :].bitcast(I32), tab_scales[0].bitcast(I32))
 
-        nc.sync.dma_start(w1_raw[:, PACK // 2 : PACK, :], w1_rows[:, PACK // 2 : PACK, :])
+        nc.sync.dma_start(w1_flat[:, FIRST_W1:], w1_rows[:, FIRST_W1:])
 
         bias_rows = keep.tile([P, P], F32, name="bias_rows", align_bytes=64)
         nc.vector.memset(bias_rows[:], 0.0)

@@ -30,7 +30,7 @@ GATE_BYTES = 4 * T
 FIRST_W1 = 768
 AHEAD = 320
 LAST = 192
-WARM_UP = (512, 256, 128)
+WARM_PASSES, WARM_COLUMNS = 3, 32
 VECTOR_GROUP = 3
 FIRST_GROUPS = 7
 H_BANKS = (2, 4, 6)
@@ -110,13 +110,13 @@ def tile_list_tabgate_bias_kernel(tc, tab_words, tab_scales, w1, w2_words, w2_sc
         nc.vector.quantize_mx(out=w1_q[:].bitcast(FP8X4), scales=w1_sc[:], in_=w1_bf[:])
 
         warm = psum.tile([P, CHUNK], F32, name="warm", tag="bank%d" % (FIRST_GROUPS - 1))
-        for width in WARM_UP:
+        for warm_pass in range(WARM_PASSES):
             nc.tensor.matmul_mx(
-                out=warm[:, 0:width],
-                lhsT=w1_q[:, 0:P].bitcast(FP8X4),
-                lhsT_scale=w1_sc[:, 0:P],
-                rhs=w1_q[:, 0:width].bitcast(FP8X4),
-                rhs_scale=w1_sc[:, 0:width],
+                out=warm[0:WARM_COLUMNS, :],
+                lhsT=w1_q[:, 0:WARM_COLUMNS].bitcast(FP8X4),
+                lhsT_scale=w1_sc[:, 0:WARM_COLUMNS],
+                rhs=w1_q[:].bitcast(FP8X4),
+                rhs_scale=w1_sc[:],
                 start=True,
                 stop=True,
             )

@@ -227,17 +227,19 @@ def tile_list_tabgate_bias_kernel(tc, tab_words, tab_scales, w1, w2_words, w2_sc
         relu(8)
         add_bias(2 * PAIR, PAIR, 0)
         gate(2 * PAIR, PAIR, 0)
+        store(0, 3 * PAIR, 0)
         relu(9)
         quantize(4)
         add_bias(3 * PAIR, PAIR, 0)
         gate(3 * PAIR, PAIR, 0)
-        store(0, 4 * PAIR, 0)
+        store(3 * PAIR, PAIR, 0)
         project(4 * PAIR, PAIR, 0)
 
         add_bias(0, CHUNK, 1)
         project(CHUNK, CHUNK, 1)
         gate(0, CHUNK, 1)
-        store(0, CHUNK, 1)
+        store(0, PAIR, 1)
+        store(PAIR, PAIR, 1)
         relu(10)
         relu(11)
         quantize(5)

from contextlib import ExitStack

import concourse.mybir as mybir

K, R, M, T, S = 512, 512, 256, 4096, 1536
FLOPS = 2 * K * R * S + 2 * R * M * S

F32 = mybir.dt.float32
BF16 = mybir.dt.bfloat16
I32 = mybir.dt.int32
U32 = mybir.dt.uint32
U16 = mybir.dt.uint16
U8 = mybir.dt.uint8
FP8X4 = mybir.dt.float8_e4m3fn_x4
FP4X4 = mybir.dt.float4_e2m1fn_x4
ACT = mybir.ActivationFunctionType
ALU = mybir.AluOpType

P = 128
PACK = 4
QUADRANT = 32
SCALE_ROWS = 4
SPREAD_FIRST, SPREAD = 32, 4
PLANE = 4
LANES = 16
CHUNK = 512
PAIR = 256
GROUP = 128
GATE_BYTES = 4 * T
FIRST_W1 = 768
AHEAD = 320
LAST = 192
WARM_PASSES, WARM_COLUMNS = 3, 32
VECTOR_GROUP = 3
FIRST_GROUPS = 7
H_BANKS = (2, 4, 6)
Y_BANKS = (3, 5, 0, 1, 7)


def tile_list_tabgate_bias_kernel(tc, tab_words, tab_scales, w1, w2_words, w2_scales, gT, b, offs, out):
    nc = tc.nc
    with ExitStack() as ctx:
        keep = ctx.enter_context(tc.tile_pool(name="keep", bufs=1))
        late = ctx.enter_context(tc.tile_pool(name="late", bufs=1))
        psum = ctx.enter_context(tc.psum_pool(name="psum", bufs=1))

        w1_raw = keep.tile([P, PACK, R], F32, name="w1_raw")
        w1_rows = w1.rearrange("(p j) c -> p (j c)", j=PACK)
        w1_flat = w1_raw[:].rearrange("p j c -> p (j c)")
        nc.sync.dma_start(w1_flat[:, 0:FIRST_W1], w1_rows[:, 0:FIRST_W1])

        offsets = keep.tile([P, S // LANES], U16, name="offsets")
        nc.sync.dma_start(offsets[:], offs)

        tab_sc = keep.tile([P, T], U8, name="tab_sc", align_bytes=64)
        nc.vector.memset(tab_sc[:].bitcast(I32), 0)
        nc.sync.dma_start(tab_sc[SPREAD_FIRST : SPREAD_FIRST + 16 * SPREAD : SPREAD, :].bitcast(I32), tab_scales[0].bitcast(I32))

        nc.sync.dma_start(w1_flat[:, FIRST_W1:], w1_rows[:, FIRST_W1:])

        bias_rows = keep.tile([P, P], F32, name="bias_rows", align_bytes=64)
        nc.vector.memset(bias_rows[:], 0.0)

        nc.sync.dma_start(
            bias_rows[0:P:QUADRANT, 0 : M // P * QUADRANT].rearrange("q (h i) -> q h i", i=QUADRANT),
            b.rearrange("(h q i) -> q h i", h=M // P, i=QUADRANT),
        )

        tab_w = keep.tile([P, T], U32, name="tab_w", align_bytes=64)
        nc.sync.dma_start(tab_w[:].bitcast(I32), tab_words[0].rearrange("p t i -> p (t i)").bitcast(I32))

        gates = [late.tile([P, T], F32, name="gate%d" % half, align_bytes=64, offset=half * GATE_BYTES) for half in range(M // P)]
        nc.sync.dma_start(gates[0][:, 0:AHEAD], gT[0:P, 0:AHEAD])

        picked_sc = late.tile([P, S], U8, name="picked_sc", align_bytes=64, offset=GATE_BYTES)
        nc.vector.tensor_copy(picked_sc[:], tab_sc[:].indirect(offsets[:]))
        v_sc = keep.tile([P, S], U8, name="v_sc", align_bytes=64)
        nc.vector.memset(v_sc[:].bitcast(I32), 0)
        for quad in (0, 2, 1, 3):
            nc.sync.dma_start(
                v_sc[QUADRANT * quad + PLANE : QUADRANT * quad + PLANE + SCALE_ROWS, :].bitcast(I32),
                picked_sc[SPREAD_FIRST + SCALE_ROWS * SPREAD * quad : SPREAD_FIRST + SCALE_ROWS * SPREAD * (quad + 1) : SPREAD, :].bitcast(I32),
            )

        w1_bf = keep.tile([P, PACK * R], BF16, name="w1_bf", align_bytes=64)
        for copy, places in ((nc.scalar.copy, slice(0, P // 2)), (nc.vector.tensor_copy, slice(P // 2, P))):
            copy(
                w1_bf[:].rearrange("p (t m j) -> p m t j", t=PACK, j=PACK)[:, places, :, :],
                w1_raw[:].rearrange("p j (m t) -> p m t j", t=PACK)[:, places, :, :],
            )

        w2_w = keep.tile([P, 2 * M], U8, name="w2_w", align_bytes=64)
        w2_sc = keep.tile([P, M], U8, name="w2_sc", align_bytes=64)
        bias = keep.tile([P, P], F32, name="bias", align_bytes=64)
        nc.vector.transpose(bias[:], bias_rows[:])

        nc.vector.memset(w2_sc[:].bitcast(I32), 0)
        nc.sync.dma_start(gates[0][:, AHEAD:T], gT[0:P, AHEAD:T])
        nc.sync.dma_start(w2_w[:].bitcast(I32), w2_words[0].bitcast(I32))
        for quad in range(P // QUADRANT):
            nc.gpsimd.dma_start(
                w2_sc[QUADRANT * quad : QUADRANT * quad + SCALE_ROWS, :].bitcast(I32),
                w2_scales[0, SCALE_ROWS * quad : SCALE_ROWS * (quad + 1), :].bitcast(I32),
            )

        nc.scalar.dma_start(gates[1][:], gT[P : 2 * P, :])

        w1_q = keep.tile([P, R], U32, name="w1_q", align_bytes=64)
        w1_sc = keep.tile([P, R], U8, name="w1_sc", align_bytes=64)
        nc.vector.quantize_mx(out=w1_q[:].bitcast(FP8X4), scales=w1_sc[:], in_=w1_bf[:])

        warm = psum.tile([P, CHUNK], F32, name="warm", tag="bank%d" % (FIRST_GROUPS - 1))
        for warm_pass in range(WARM_PASSES):
            nc.tensor.matmul_mx(
                out=warm[0:WARM_COLUMNS, :],
                lhsT=w1_q[:, 0:WARM_COLUMNS].bitcast(FP8X4),
                lhsT_scale=w1_sc[:, 0:WARM_COLUMNS],
                rhs=w1_q[:].bitcast(FP8X4),
                rhs_scale=w1_sc[:],
                start=True,
                stop=True,
            )

        def listed(first, width):
            return offsets[:, first // LANES : (first + width) // LANES]

        v_w = []
        for c in range(S // CHUNK):
            words = keep.tile([P, CHUNK], U32, name="v_w%d" % c, tag="v_w%d" % c, align_bytes=64)
            nc.vector.tensor_copy(words[:], tab_w[:].indirect(listed(c * CHUNK, CHUNK)))
            v_w.append(words)

        h_bf = [keep.tile([P, PACK * PAIR], BF16, name="h_bf%d" % pair, align_bytes=64) for pair in range(S // PAIR)]
        h_q = [keep.tile([P, CHUNK], U32, name="h_q%d" % c, align_bytes=64) for c in range(S // CHUNK)]
        h_sc = [keep.tile([P, CHUNK], U8, name="h_sc%d" % c, align_bytes=64) for c in range(S // CHUNK)]
        results = [keep.tile([P, S], F32, name="res%d" % half, align_bytes=64) for half in range(M // P)]
        h_ps = {}
        y_ps = {}
        y_sb = {}

        def h_bank(group):
            return group if group < FIRST_GROUPS else H_BANKS[(group - FIRST_GROUPS) % len(H_BANKS)]

        def hidden(group):
            c, i = divmod(group * GROUP, CHUNK)
            bank = psum.tile([P, PACK, GROUP], F32, name="h_bank", tag="bank%d" % h_bank(group))
            for t in range(PACK):
                nc.tensor.matmul_mx(
                    out=bank[:, t, :],
                    lhsT=w1_q[:, t * P : (t + 1) * P].bitcast(FP8X4),
                    lhsT_scale=w1_sc[:, t * P : (t + 1) * P],
                    rhs=v_w[c][:, i : i + GROUP].bitcast(FP8X4),
                    rhs_scale=v_sc[PLANE:P, group * GROUP : (group + 1) * GROUP],
                    start=True,
                    stop=True,
                )
            h_ps[group] = bank

        def relu(group):
            pair, i = divmod(group * GROUP, PAIR)
            dst = h_bf[pair][:, PACK * i : PACK * (i + GROUP)].rearrange("p (n t) -> p n t", t=PACK)
            src = h_ps[group][:].rearrange("p t n -> p n t")
            if group == VECTOR_GROUP:
                nc.vector.tensor_scalar_max(dst, src, 0.0)
            else:
                nc.scalar.activation(dst, src, ACT.Relu)
            following = len(h_ps)
            if following < S // GROUP and h_bank(following) == h_bank(group):
                hidden(following)

        def quantize(pair):
            c, i = divmod(pair * PAIR, CHUNK)
            nc.vector.quantize_mx(out=h_q[c][:, i : i + PAIR].bitcast(FP8X4), scales=h_sc[c][:, i : i + PAIR], in_=h_bf[pair][:])

        def project(first, width, half):
            c, i = divmod(first, CHUNK)
            bank = psum.tile([P, CHUNK], F32, name="y_bank", tag="bank%d" % Y_BANKS[len(y_ps) % len(Y_BANKS)])
            nc.tensor.matmul_mx(
                out=bank[:, 0:width],
                lhsT=w2_w[:, 2 * half * P : 2 * (half + 1) * P].bitcast(FP4X4),
                lhsT_scale=w2_sc[:, half * P : (half + 1) * P],
                rhs=h_q[c][:, i : i + width].bitcast(FP8X4),
                rhs_scale=h_sc[c][:, i : i + width],
                start=True,
                stop=True,
            )
            y_ps[first, half] = bank[:, 0:width]

        def add_bias(first, width, half):
            y = keep.tile([P, width], F32, name="y%d_%d" % (first, half), align_bytes=64)
            nc.scalar.activation(y[:], y_ps[first, half], ACT.Identity, bias=bias[:, QUADRANT * half : QUADRANT * half + 1])
            y_sb[first, half] = y

        def gate(first, width, half, skip=0):
            token = first + skip
            nc.vector.tensor_tensor(
                results[half][:, token : token + width],
                gates[half][:].indirect(listed(token, width)),
                y_sb[first, half][:, skip : skip + width],
                ALU.mult,
            )

        def store(first, width, half):
            nc.sync.dma_start(out[half * P : (half + 1) * P, first : first + width], results[half][:, first : first + width])

        for group in range(FIRST_GROUPS):
            hidden(group)
        for group in range(CHUNK // GROUP):
            relu(group)
        quantize(0)
        quantize(1)

        picked = keep.tile([P, CHUNK], F32, name="picked", tag="v_w1", align_bytes=64)
        nc.vector.tensor_copy(picked[:], gates[0][:].indirect(listed(0, CHUNK)))
        relu(4)
        project(0, CHUNK, 1)
        relu(5)
        project(0, CHUNK, 0)
        quantize(2)
        relu(6)
        project(2 * PAIR, PAIR, 0)
        nc.vector.scalar_tensor_tensor(results[0][:, 0:CHUNK], y_ps[0, 0], bias[:, 0:1], picked[:], ALU.add, ALU.mult)
        relu(7)
        quantize(3)
        project(3 * PAIR, PAIR, 0)

        relu(8)
        add_bias(2 * PAIR, PAIR, 0)
        gate(2 * PAIR, PAIR, 0)
        store(0, 3 * PAIR, 0)
        relu(9)
        quantize(4)
        add_bias(3 * PAIR, PAIR, 0)
        gate(3 * PAIR, PAIR, 0)
        store(3 * PAIR, PAIR, 0)
        project(4 * PAIR, PAIR, 0)

        add_bias(0, CHUNK, 1)
        project(CHUNK, CHUNK, 1)
        gate(0, CHUNK, 1)
        store(0, PAIR, 1)
        store(PAIR, PAIR, 1)
        relu(10)
        relu(11)
        quantize(5)
        project(5 * PAIR, PAIR, 0)
        project(2 * CHUNK, CHUNK, 1)
        add_bias(4 * PAIR, PAIR, 0)
        gate(4 * PAIR, PAIR, 0)
        store(4 * PAIR, PAIR, 0)
        add_bias(CHUNK, CHUNK, 1)
        gate(CHUNK, CHUNK, 1)
        store(CHUNK, CHUNK, 1)
        add_bias(5 * PAIR, PAIR, 0)
        gate(5 * PAIR, PAIR, 0)
        store(5 * PAIR, PAIR, 0)
        add_bias(2 * CHUNK, CHUNK, 1)
        for skip, width in ((0, CHUNK - LAST), (CHUNK - LAST, LAST)):
            gate(2 * CHUNK, width, 1, skip)
            store(2 * CHUNK + skip, width, 1)
